import numpy as np
import ml_dtypes


def mxq(x, axis, fmt="e4m3"):
    dtype, down = {"e4m3": (ml_dtypes.float8_e4m3fn, 7), "e5m2": (ml_dtypes.float8_e5m2, 14)}[fmt]
    v = np.moveaxis(np.asarray(x, np.float32).astype(ml_dtypes.bfloat16).astype(np.float64), axis, -1)
    blocks = v.reshape(v.shape[:-1] + (-1, 32))
    amax = np.abs(blocks).max(-1, keepdims=True)
    byte = np.maximum(np.where(amax > 0, np.frexp(amax)[1] - 1 + 127, 0) - down, 1)
    scale = np.exp2(byte - 127.0)
    codes = (blocks / scale).astype(np.float32).astype(dtype).astype(np.float64)
    return np.moveaxis((codes * scale).reshape(v.shape), -1, axis)


WIDE = False


def mx_kscale(k):
    if not WIDE:
        return np.ones(k)
    levels = np.array([10, -10, 5, -5, 0])
    if k % 512:
        return np.exp2(np.random.permutation(np.resize(levels, k // 32))).repeat(32)
    a = np.empty((k // 512, 16))
    for p in range(k // 512):
        a[p, :8] = np.random.permutation(np.resize(levels, 8))
        for g in range(8):
            far = levels[np.abs(levels - a[p, g]) >= 10]
            a[p, g + 8] = far[np.random.randint(len(far))]
    return np.exp2(a.ravel()).repeat(32)


def f64(x):
    return np.asarray(x).astype(np.float64)


def striped(idx):
    return np.tile(idx.reshape(-1, 16).T, (8, 1)).astype(np.uint16)


def unstriped(offs):
    return offs[:16].T.reshape(-1).astype(np.int64)


def striped8(idx):
    return np.concatenate([x.reshape(-1, 16).T for x in idx]).astype(np.uint16)


def runs(offs, k):
    lists = np.stack([offs[16 * r : 16 * r + 16].T.reshape(-1) for r in range(8)]).astype(np.int64)
    return lists[np.arange(k) % 512 // 64]


def pack_weight(w):
    k, n = w.shape
    w = f64(np.asarray(w, np.float32).astype(ml_dtypes.bfloat16)).reshape(k // 32, 32, n)
    amax = np.abs(w).max(1)
    byte = np.clip(np.where(amax > 0, np.frexp(amax)[1] - 1 + 127 - 7, 1), 1, 254)
    scaled = (w * np.exp2(127.0 - byte)[:, None, :]).reshape(k, n).astype(np.float32)
    words = np.ascontiguousarray(scaled.reshape(k // 512, 128, 4, n).transpose(0, 1, 3, 2)).astype(ml_dtypes.float8_e4m3fn).view(np.uint8)
    return words, np.ascontiguousarray(byte.astype(np.uint8).reshape(k // 512, 16, n))


def unpack_weight(words, scales):
    g, p, n, _ = words.shape
    vals = np.ascontiguousarray(words).view(ml_dtypes.float8_e4m3fn).astype(np.float64) * np.repeat(np.exp2(scales.astype(np.float64) - 127.0), 8, axis=1)[..., None]
    return vals.transpose(0, 1, 3, 2).reshape(g * 512, n)


K, T, S, V, N, H = 512, 2048, 512, 256, 512, 512


def setup_inputs():
    n = np.random.standard_normal
    s = mx_kscale(K)[:, None]
    u = mx_kscale(H)
    packed_xT = pack_weight(n((K, T)) * s)
    return {
        "x_words": packed_xT[0],
        "x_scales": packed_xT[1],
        "w1": (n((K, H)) / np.sqrt(K) / s * u).astype(np.float32),
        "sg1": np.sign(n((H, V))).astype(np.float32),
        "sg2": np.sign(n((H, V))).astype(np.float32),
        "sg3": np.sign(n((H, V))).astype(np.float32),
        "w2": (n((H, N)) / np.sqrt(H) / u[:, None]).astype(np.float32),
        "offs": striped(np.random.permutation(T)[:S]),
        "h1": striped8(np.stack([np.random.permutation(S)[:V] for _ in range(8)])),
        "h2": striped8(np.stack([np.random.permutation(S)[:V] for _ in range(8)])),
        "h3": striped8(np.stack([np.random.permutation(S)[:V] for _ in range(8)])),
    }


def reference(x_words, x_scales, w1, sg1, sg2, sg3, w2, offs, h1, h2, h3):
    xq = unpack_weight(x_words, x_scales)[:, unstriped(offs)]
    y = mxq(f64(w1), 0, "e4m3").T @ xq
    t1 = f64(sg1) * (y[np.arange(H)[:, None], runs(h1, H)])
    t2 = f64(sg2) * (y[np.arange(H)[:, None], runs(h2, H)])
    t3 = f64(sg3) * (y[np.arange(H)[:, None], runs(h3, H)])
    z = np.maximum(np.minimum(t1, t2), np.minimum(np.maximum(t1, t2), t3))
    return mxq(f64(w2), 0, "e4m3").T @ mxq(z, 0, "e4m3")

@@ -1,0 +1,177 @@
+from contextlib import ExitStack
+
+import concourse.mybir as mybir
+
+K, T, S, V, N, H = 512, 2048, 512, 256, 512, 512
+FLOPS = 2 * K * H * S + 2 * H * N * V
+
+F32 = mybir.dt.float32
+BF16 = mybir.dt.bfloat16
+I32 = mybir.dt.int32
+U32 = mybir.dt.uint32
+U16 = mybir.dt.uint16
+U8 = mybir.dt.uint8
+FP8X4 = mybir.dt.float8_e4m3fn_x4
+MULT = mybir.AluOpType.mult
+MIN = mybir.AluOpType.min
+MAX = mybir.AluOpType.max
+
+P = 128
+PACK = 4
+W1_VECTOR_ROWS = 80
+VH = V // 2
+SH = S // 2
+
+
+def tile_picked_csketch_none_p_kernel(tc, x_words, x_scales, w1, sg1, sg2, sg3, w2, offs, h1, h2, h3, out):
+    nc = tc.nc
+    with ExitStack() as ctx:
+        sb = ctx.enter_context(tc.tile_pool(name="sb", bufs=1))
+        ps = ctx.enter_context(tc.psum_pool(name="ps", bufs=1))
+
+        offs_sb = sb.tile([P, S // 16], U16, name="offs_sb")
+        h_sb = [sb.tile([P, V // 16], U16, name="h%d_sb" % n) for n in range(3)]
+        xw = sb.tile([P, T], U32, name="xw", align_bytes=64)
+        xs = sb.tile([P, T], U8, name="xs", align_bytes=64)
+        w1_raw = sb.tile([P, PACK, H], F32, name="w1_raw", align_bytes=64)
+        w2_raw = sb.tile([P, PACK, N], F32, name="w2_raw", align_bytes=64)
+        sg_sb = [sb.tile([P, PACK, V], F32, name="sg%d_sb" % n, align_bytes=64) for n in range(3)]
+
+        nc.vector.memset(xs[:].bitcast(I32), 0)
+        nc.sync.dma_start(offs_sb[:], offs)
+        nc.sync.dma_start(w1_raw[:], w1.rearrange("(p j) c -> p j c", j=PACK))
+        nc.sync.dma_start(xw[:].bitcast(I32), x_words[0].rearrange("p n t -> p (n t)").bitcast(I32))
+        for q in range(4):
+            nc.scalar.dma_start(xs[32 * q : 32 * q + 4, :].bitcast(I32), x_scales[0, 4 * q : 4 * q + 4, :].bitcast(I32))
+        for n, (h, sg) in enumerate(((h1, sg1), (h2, sg2), (h3, sg3))):
+            nc.sync.dma_start(h_sb[n][:], h)
+            nc.sync.dma_start(sg_sb[n][:], sg.rearrange("(p t) v -> p t v", t=PACK))
+        nc.sync.dma_start(w2_raw[:], w2.rearrange("(p j) c -> p j c", j=PACK))
+
+        gs = sb.tile([P, S], U8, name="gs", align_bytes=64)
+        nc.vector.tensor_copy(gs[:], xs[:].indirect(offs_sb[:]))
+
+        w1_bf = sb.tile([P, PACK, P, PACK], BF16, name="w1_bf", align_bytes=64)
+        src = w1_raw[:].rearrange("p j (m t) -> p m j t", t=PACK)
+        dst = w1_bf[:].rearrange("p t m j -> p m j t")
+        nc.vector.tensor_copy(dst[:, :W1_VECTOR_ROWS], src[:, :W1_VECTOR_ROWS])
+        nc.scalar.copy(dst[:, W1_VECTOR_ROWS:], src[:, W1_VECTOR_ROWS:])
+        w1_codes = sb.tile([P, H], U32, name="w1_codes", align_bytes=64)
+        w1_scales = sb.tile([P, H], U8, name="w1_scales", align_bytes=64)
+        nc.vector.quantize_mx(out=w1_codes[:].bitcast(FP8X4), scales=w1_scales[:], in_=w1_bf[:].rearrange("p t m j -> p (t m j)"))
+
+        gw = sb.tile([P, S], U32, name="gw", align_bytes=64)
+        for half in range(2):
+            nc.vector.tensor_copy(gw[:, half * SH : (half + 1) * SH], xw[:].indirect(offs_sb[:, half * SH // 16 : (half + 1) * SH // 16]))
+
+        def first_product(acc, t, cols):
+            nc.tensor.matmul_mx(
+                out=acc,
+                lhsT=w1_codes[:, t * P : (t + 1) * P].bitcast(FP8X4),
+                lhsT_scale=w1_scales[:, t * P : (t + 1) * P],
+                rhs=gw[:, cols].bitcast(FP8X4),
+                rhs_scale=gs[:, cols],
+                start=True,
+                stop=True,
+            )
+
+        y = [sb.tile([P, S], F32, name="y%d" % t, align_bytes=64) for t in range(PACK)]
+        for half in range(2):
+            acc = ps.tile([P, SH], F32, name="y0_ps%d" % half)
+            cols = slice(half * SH, (half + 1) * SH)
+            first_product(acc[:], 0, cols)
+            if half == 0:
+                nc.scalar.copy(y[0][:, cols], acc[:])
+            else:
+                nc.vector.tensor_copy(y[0][:, cols], acc[:])
+        for t in range(1, PACK):
+            acc = ps.tile([P, S], F32, name="y_ps%d" % t)
+            first_product(acc[:], t, slice(0, S))
+            nc.scalar.copy(y[t][:], acc[:])
+
+        w2_bf = [sb.tile([P, P, PACK], BF16, name="w2_bf%d" % u, align_bytes=64) for u in range(PACK)]
+        w2_codes = [sb.tile([P, P], U32, name="w2_codes%d" % u, align_bytes=64) for u in range(PACK)]
+        w2_scales = [sb.tile([P, P], U8, name="w2_scales%d" % u, align_bytes=64) for u in range(PACK)]
+        for u in range(PACK):
+            nc.scalar.copy(
+                w2_bf[u][:].rearrange("p (c i) j -> p c j i", i=4),
+                w2_raw[:, :, u * P : (u + 1) * P].rearrange("p j (c i) -> p c j i", i=4),
+            )
+
+        def quantize_w2(u):
+            nc.vector.quantize_mx(out=w2_codes[u][:].bitcast(FP8X4), scales=w2_scales[u][:], in_=w2_bf[u][:].rearrange("p m j -> p (m j)"))
+
+        t12 = [sb.tile([P, PACK, V], F32, name="t%d" % n, align_bytes=64) for n in range(2)]
+        for n in range(2):
+            for t in range(PACK):
+                nc.vector.tensor_tensor(t12[n][:, t, :], y[t][:].indirect(h_sb[n][:]), sg_sb[n][:, t, :], MULT)
+        t3 = [sb.tile([P, PACK, VH], F32, name="t3_%d" % half, align_bytes=64) for half in range(2)]
+
+        def third(half, t):
+            nc.vector.tensor_tensor(
+                t3[half][:, t, :],
+                y[t][:].indirect(h_sb[2][:, half * VH // 16 : (half + 1) * VH // 16]),
+                sg_sb[2][:, t, half * VH : (half + 1) * VH],
+                MULT,
+            )
+
+        lo = sb.tile([P, PACK, V], F32, name="lo", align_bytes=64)
+        hi = sb.tile([P, PACK, V], F32, name="hi", align_bytes=64)
+        mid = [sb.tile([P, PACK, VH], F32, name="mid%d" % half, align_bytes=64) for half in range(2)]
+        z_bf = [sb.tile([P, VH, PACK], BF16, name="z_bf%d" % half, align_bytes=64) for half in range(2)]
+        z_codes = [sb.tile([P, VH], U32, name="z_codes%d" % half, align_bytes=64) for half in range(2)]
+        z_scales = [sb.tile([P, VH], U8, name="z_scales%d" % half, align_bytes=64) for half in range(2)]
+
+        def clip_above(half):
+            nc.vector.tensor_tensor(mid[half][:], hi[:, :, half * VH : (half + 1) * VH], t3[half][:], MIN)
+
+        def clip_below(half):
+            nc.vector.tensor_tensor(
+                z_bf[half][:].rearrange("p (c i) t -> p c t i", i=4),
+                lo[:, :, half * VH : (half + 1) * VH].rearrange("p t (c i) -> p c t i", i=4),
+                mid[half][:].rearrange("p t (c i) -> p c t i", i=4),
+                MAX,
+            )
+
+        def quantize_z(half):
+            nc.vector.quantize_mx(out=z_codes[half][:].bitcast(FP8X4), scales=z_scales[half][:], in_=z_bf[half][:].rearrange("p v t -> p (v t)"))
+
+        out_rows = out.rearrange("(u p) v -> p u v", p=P)
+
+        def second_product(half, u0, count, copy_engine, store_engine):
+            acc = ps.tile([P, count, VH], F32, name="o_ps%d_%d" % (half, u0))
+            for u in range(u0, u0 + count):
+                nc.tensor.matmul_mx(
+                    out=acc[:, u - u0, :],
+                    lhsT=w2_codes[u][:].bitcast(FP8X4),
+                    lhsT_scale=w2_scales[u][:],
+                    rhs=z_codes[half][:].bitcast(FP8X4),
+                    rhs_scale=z_scales[half][:],
+                    start=True,
+                    stop=True,
+                )
+            res = sb.tile([P, count, VH], F32, name="res%d_%d" % (half, u0), align_bytes=64)
+            copy_engine(res[:], acc[:])
+            store_engine.dma_start(out_rows[:, u0 : u0 + count, half * VH : (half + 1) * VH], res[:])
+
+        for t in range(PACK):
+            third(0, t)
+        nc.vector.tensor_tensor(hi[:], t12[0][:], t12[1][:], MAX)
+        nc.vector.tensor_tensor(lo[:], t12[0][:], t12[1][:], MIN)
+        clip_above(0)
+        third(1, 0)
+        quantize_w2(0)
+        quantize_w2(1)
+        clip_below(0)
+        third(1, 1)
+        quantize_w2(2)
+        quantize_w2(3)
+        quantize_z(0)
+        second_product(0, 0, PACK, nc.scalar.copy, nc.sync)
+        third(1, 2)
+        third(1, 3)
+        clip_above(1)
+        clip_below(1)
+        quantize_z(1)
+        second_product(1, 0, 2, nc.scalar.copy, nc.scalar)
+        second_product(1, 2, 2, nc.vector.tensor_copy, nc.sync)

@@ -18,7 +18,7 @@ MAX = mybir.AluOpType.max
 
 P = 128
 PACK = 4
-W1_VECTOR_ROWS = 80
+W1_VECTOR_ROWS = 64
 VH = V // 2
 SH = S // 2
 
@@ -40,9 +40,9 @@ def tile_picked_csketch_none_p_kernel(tc, x_words, x_scales, w1, sg1, sg2, sg3, 
         nc.vector.memset(xs[:].bitcast(I32), 0)
         nc.sync.dma_start(offs_sb[:], offs)
         nc.sync.dma_start(w1_raw[:], w1.rearrange("(p j) c -> p j c", j=PACK))
-        nc.sync.dma_start(xw[:].bitcast(I32), x_words[0].rearrange("p n t -> p (n t)").bitcast(I32))
         for q in range(4):
-            nc.scalar.dma_start(xs[32 * q : 32 * q + 4, :].bitcast(I32), x_scales[0, 4 * q : 4 * q + 4, :].bitcast(I32))
+            nc.sync.dma_start(xs[32 * q : 32 * q + 4, :].bitcast(I32), x_scales[0, 4 * q : 4 * q + 4, :].bitcast(I32))
+        nc.sync.dma_start(xw[:].bitcast(I32), x_words[0].rearrange("p n t -> p (n t)").bitcast(I32))
         for n, (h, sg) in enumerate(((h1, sg1), (h2, sg2), (h3, sg3))):
             nc.sync.dma_start(h_sb[n][:], h)
             nc.sync.dma_start(sg_sb[n][:], sg.rearrange("(p t) v -> p t v", t=PACK))
@@ -52,8 +52,8 @@ def tile_picked_csketch_none_p_kernel(tc, x_words, x_scales, w1, sg1, sg2, sg3, 
         nc.vector.tensor_copy(gs[:], xs[:].indirect(offs_sb[:]))
 
         w1_bf = sb.tile([P, PACK, P, PACK], BF16, name="w1_bf", align_bytes=64)
-        src = w1_raw[:].rearrange("p j (m t) -> p m j t", t=PACK)
-        dst = w1_bf[:].rearrange("p t m j -> p m j t")
+        src = w1_raw[:].rearrange("p j (m t) -> p m t j", t=PACK)
+        dst = w1_bf[:].rearrange("p t m j -> p m t j")
         nc.vector.tensor_copy(dst[:, :W1_VECTOR_ROWS], src[:, :W1_VECTOR_ROWS])
         nc.scalar.copy(dst[:, W1_VECTOR_ROWS:], src[:, W1_VECTOR_ROWS:])
         w1_codes = sb.tile([P, H], U32, name="w1_codes", align_bytes=64)
@@ -94,8 +94,8 @@ def tile_picked_csketch_none_p_kernel(tc, x_words, x_scales, w1, sg1, sg2, sg3, 
         w2_scales = [sb.tile([P, P], U8, name="w2_scales%d" % u, align_bytes=64) for u in range(PACK)]
         for u in range(PACK):
             nc.scalar.copy(
-                w2_bf[u][:].rearrange("p (c i) j -> p c j i", i=4),
-                w2_raw[:, :, u * P : (u + 1) * P].rearrange("p j (c i) -> p c j i", i=4),
+                w2_bf[u][:],
+                w2_raw[:, :, u * P : (u + 1) * P].rearrange("p j c -> p c j"),
             )
 
         def quantize_w2(u):
@@ -126,12 +126,17 @@ def tile_picked_csketch_none_p_kernel(tc, x_words, x_scales, w1, sg1, sg2, sg3, 
             nc.vector.tensor_tensor(mid[half][:], hi[:, :, half * VH : (half + 1) * VH], t3[half][:], MIN)
 
         def clip_below(half):
-            nc.vector.tensor_tensor(
-                z_bf[half][:].rearrange("p (c i) t -> p c t i", i=4),
-                lo[:, :, half * VH : (half + 1) * VH].rearrange("p t (c i) -> p c t i", i=4),
-                mid[half][:].rearrange("p t (c i) -> p c t i", i=4),
-                MAX,
-            )
+            if half == 0:
+                z_f32 = sb.tile([P, PACK, VH], F32, name="z_f32", align_bytes=64)
+                nc.vector.tensor_tensor(z_f32[:], lo[:, :, :VH], mid[0][:], MAX)
+                nc.scalar.copy(z_bf[0][:], z_f32[:].rearrange("p t v -> p v t"))
+            else:
+                nc.vector.tensor_tensor(
+                    z_bf[1][:],
+                    lo[:, :, VH:].rearrange("p t v -> p v t"),
+                    mid[1][:].rearrange("p t v -> p v t"),
+                    MAX,
+                )
 
         def quantize_z(half):
             nc.vector.quantize_mx(out=z_codes[half][:].bitcast(FP8X4), scales=z_scales[half][:], in_=z_bf[half][:].rearrange("p v t -> p (v t)"))
@@ -166,9 +171,9 @@ def tile_picked_csketch_none_p_kernel(tc, x_words, x_scales, w1, sg1, sg2, sg3, 
         third(1, 1)
         quantize_w2(2)
         quantize_w2(3)
+        third(1, 2)
         quantize_z(0)
         second_product(0, 0, PACK, nc.scalar.copy, nc.sync)
-        third(1, 2)
         third(1, 3)
         clip_above(1)
         clip_below(1)

@@ -18,7 +18,7 @@ MAX = mybir.AluOpType.max
 
 P = 128
 PACK = 4
-W1_VECTOR_ROWS = 64
+W1_VECTOR_ROWS = 48
 VH = V // 2
 SH = S // 2
 
@@ -38,15 +38,16 @@ def tile_picked_csketch_none_p_kernel(tc, x_words, x_scales, w1, sg1, sg2, sg3, 
         sg_sb = [sb.tile([P, PACK, V], F32, name="sg%d_sb" % n, align_bytes=64) for n in range(3)]
 
         nc.vector.memset(xs[:].bitcast(I32), 0)
-        nc.sync.dma_start(offs_sb[:], offs)
         nc.sync.dma_start(w1_raw[:], w1.rearrange("(p j) c -> p j c", j=PACK))
+        nc.sync.dma_start(offs_sb[:], offs)
         for q in range(4):
-            nc.sync.dma_start(xs[32 * q : 32 * q + 4, :].bitcast(I32), x_scales[0, 4 * q : 4 * q + 4, :].bitcast(I32))
+            nc.sync.dma_start(xs[q:P:32, :].bitcast(I32), x_scales[0, q:16:4, :].bitcast(I32))
         nc.sync.dma_start(xw[:].bitcast(I32), x_words[0].rearrange("p n t -> p (n t)").bitcast(I32))
         for n, (h, sg) in enumerate(((h1, sg1), (h2, sg2), (h3, sg3))):
             nc.sync.dma_start(h_sb[n][:], h)
+            if n == 1:
+                nc.sync.dma_start(w2_raw[:], w2.rearrange("(p j) c -> p j c", j=PACK))
             nc.sync.dma_start(sg_sb[n][:], sg.rearrange("(p t) v -> p t v", t=PACK))
-        nc.sync.dma_start(w2_raw[:], w2.rearrange("(p j) c -> p j c", j=PACK))
 
         gs = sb.tile([P, S], U8, name="gs", align_bytes=64)
         nc.vector.tensor_copy(gs[:], xs[:].indirect(offs_sb[:]))
@@ -58,11 +59,22 @@ def tile_picked_csketch_none_p_kernel(tc, x_words, x_scales, w1, sg1, sg2, sg3, 
         nc.scalar.copy(dst[:, W1_VECTOR_ROWS:], src[:, W1_VECTOR_ROWS:])
         w1_codes = sb.tile([P, H], U32, name="w1_codes", align_bytes=64)
         w1_scales = sb.tile([P, H], U8, name="w1_scales", align_bytes=64)
-        nc.vector.quantize_mx(out=w1_codes[:].bitcast(FP8X4), scales=w1_scales[:], in_=w1_bf[:].rearrange("p t m j -> p (t m j)"))
+
+        def quantize_w1(pair):
+            cols = slice(2 * pair * P, 2 * (pair + 1) * P)
+            nc.vector.quantize_mx(
+                out=w1_codes[:, cols].bitcast(FP8X4),
+                scales=w1_scales[:, cols],
+                in_=w1_bf[:, 2 * pair : 2 * pair + 2].rearrange("p t m j -> p (t m j)"),
+            )
+
+        quantize_w1(0)
 
         gw = sb.tile([P, S], U32, name="gw", align_bytes=64)
         for half in range(2):
             nc.vector.tensor_copy(gw[:, half * SH : (half + 1) * SH], xw[:].indirect(offs_sb[:, half * SH // 16 : (half + 1) * SH // 16]))
+
+        quantize_w1(1)
 
         def first_product(acc, t, cols):
             nc.tensor.matmul_mx(
@@ -76,18 +88,19 @@ def tile_picked_csketch_none_p_kernel(tc, x_words, x_scales, w1, sg1, sg2, sg3, 
             )
 
         y = [sb.tile([P, S], F32, name="y%d" % t, align_bytes=64) for t in range(PACK)]
-        for half in range(2):
-            acc = ps.tile([P, SH], F32, name="y0_ps%d" % half)
-            cols = slice(half * SH, (half + 1) * SH)
-            first_product(acc[:], 0, cols)
-            if half == 0:
-                nc.scalar.copy(y[0][:, cols], acc[:])
-            else:
-                nc.vector.tensor_copy(y[0][:, cols], acc[:])
-        for t in range(1, PACK):
-            acc = ps.tile([P, S], F32, name="y_ps%d" % t)
-            first_product(acc[:], t, slice(0, S))
-            nc.scalar.copy(y[t][:], acc[:])
+        pieces = (
+            (0, 0, 256, nc.scalar.copy),
+            (1, 0, 256, nc.scalar.copy),
+            (0, 256, 384, nc.scalar.copy),
+            (0, 384, 512, nc.vector.tensor_copy),
+            (1, 256, 512, nc.scalar.copy),
+            (2, 0, 512, nc.scalar.copy),
+            (3, 0, 512, nc.scalar.copy),
+        )
+        for n, (t, c0, c1, copy) in enumerate(pieces):
+            acc = ps.tile([P, c1 - c0], F32, name="y_ps%d" % n, tag="bank%d" % n)
+            first_product(acc[:], t, slice(c0, c1))
+            copy(y[t][:, c0:c1], acc[:])
 
         w2_bf = [sb.tile([P, P, PACK], BF16, name="w2_bf%d" % u, align_bytes=64) for u in range(PACK)]
         w2_codes = [sb.tile([P, P], U32, name="w2_codes%d" % u, align_bytes=64) for u in range(PACK)]
@@ -122,12 +135,13 @@ def tile_picked_csketch_none_p_kernel(tc, x_words, x_scales, w1, sg1, sg2, sg3, 
         z_codes = [sb.tile([P, VH], U32, name="z_codes%d" % half, align_bytes=64) for half in range(2)]
         z_scales = [sb.tile([P, VH], U8, name="z_scales%d" % half, align_bytes=64) for half in range(2)]
 
+        z_f32 = sb.tile([P, PACK, VH], F32, name="z_f32", align_bytes=64)
+
         def clip_above(half):
             nc.vector.tensor_tensor(mid[half][:], hi[:, :, half * VH : (half + 1) * VH], t3[half][:], MIN)
 
         def clip_below(half):
             if half == 0:
-                z_f32 = sb.tile([P, PACK, VH], F32, name="z_f32", align_bytes=64)
                 nc.vector.tensor_tensor(z_f32[:], lo[:, :, :VH], mid[0][:], MAX)
                 nc.scalar.copy(z_bf[0][:], z_f32[:].rearrange("p t v -> p v t"))
             else:
@@ -143,8 +157,8 @@ def tile_picked_csketch_none_p_kernel(tc, x_words, x_scales, w1, sg1, sg2, sg3, 
 
         out_rows = out.rearrange("(u p) v -> p u v", p=P)
 
-        def second_product(half, u0, count, copy_engine, store_engine):
-            acc = ps.tile([P, count, VH], F32, name="o_ps%d_%d" % (half, u0))
+        def second_product(half, u0, count, bank, copy_engine, store_engine):
+            acc = ps.tile([P, count, VH], F32, name="o_ps%d_%d" % (half, u0), tag="bank%d" % bank)
             for u in range(u0, u0 + count):
                 nc.tensor.matmul_mx(
                     out=acc[:, u - u0, :],
@@ -159,24 +173,48 @@ def tile_picked_csketch_none_p_kernel(tc, x_words, x_scales, w1, sg1, sg2, sg3, 
             copy_engine(res[:], acc[:])
             store_engine.dma_start(out_rows[:, u0 : u0 + count, half * VH : (half + 1) * VH], res[:])
 
+        VQ = VH // 2
+
+        def clip_above_q(q):
+            nc.vector.tensor_tensor(mid[1][:, :, q * VQ : (q + 1) * VQ], hi[:, :, VH + q * VQ : VH + (q + 1) * VQ], t3[1][:, :, q * VQ : (q + 1) * VQ], MIN)
+
+        def clip_below_q(q):
+            nc.vector.tensor_tensor(
+                z_bf[1][:, q * VQ : (q + 1) * VQ, :],
+                lo[:, :, VH + q * VQ : VH + (q + 1) * VQ].rearrange("p t v -> p v t"),
+                mid[1][:, :, q * VQ : (q + 1) * VQ].rearrange("p t v -> p v t"),
+                MAX,
+            )
+
+        def quantize_z_q(q):
+            nc.vector.quantize_mx(
+                out=z_codes[1][:, q * VQ : (q + 1) * VQ].bitcast(FP8X4),
+                scales=z_scales[1][:, q * VQ : (q + 1) * VQ],
+                in_=z_bf[1][:, q * VQ : (q + 1) * VQ, :].rearrange("p v t -> p (v t)"),
+            )
+
+        def bounds(half):
+            cols = slice(half * VH, (half + 1) * VH)
+            nc.vector.tensor_tensor(hi[:, :, cols], t12[0][:, :, cols], t12[1][:, :, cols], MAX)
+            nc.vector.tensor_tensor(lo[:, :, cols], t12[0][:, :, cols], t12[1][:, :, cols], MIN)
+
         for t in range(PACK):
             third(0, t)
-        nc.vector.tensor_tensor(hi[:], t12[0][:], t12[1][:], MAX)
-        nc.vector.tensor_tensor(lo[:], t12[0][:], t12[1][:], MIN)
+        bounds(0)
         clip_above(0)
-        third(1, 0)
-        quantize_w2(0)
-        quantize_w2(1)
+        for u in range(PACK):
+            quantize_w2(u)
         clip_below(0)
-        third(1, 1)
-        quantize_w2(2)
-        quantize_w2(3)
-        third(1, 2)
+        bounds(1)
         quantize_z(0)
-        second_product(0, 0, PACK, nc.scalar.copy, nc.sync)
-        third(1, 3)
-        clip_above(1)
-        clip_below(1)
-        quantize_z(1)
-        second_product(1, 0, 2, nc.scalar.copy, nc.scalar)
-        second_product(1, 2, 2, nc.vector.tensor_copy, nc.sync)
+        second_product(0, 0, PACK, 7, nc.scalar.copy, nc.sync)
+        for t in range(PACK):
+            third(1, t)
+        for step in (clip_above_q, clip_below_q, quantize_z_q):
+            for q in range(2):
+                step(q)
+        for u in range(PACK):
+            if u % 2 == 0:
+                second_product(1, u, 1, u, nc.scalar.copy, nc.scalar)
+            else:
+                second_product(1, u, 1, u, nc.vector.tensor_copy, nc.sync)

@@ -114,19 +114,11 @@ def tile_picked_csketch_none_p_kernel(tc, x_words, x_scales, w1, sg1, sg2, sg3, 
         def quantize_w2(u):
             nc.vector.quantize_mx(out=w2_codes[u][:].bitcast(FP8X4), scales=w2_scales[u][:], in_=w2_bf[u][:].rearrange("p m j -> p (m j)"))
 
-        t12 = [sb.tile([P, PACK, V], F32, name="t%d" % n, align_bytes=64) for n in range(2)]
-        for n in range(2):
+        t12 = [sb.tile([P, PACK, V], F32, name="t%d" % n, align_bytes=64) for n in range(3)]
+        for n in range(3):
             for t in range(PACK):
                 nc.vector.tensor_tensor(t12[n][:, t, :], y[t][:].indirect(h_sb[n][:]), sg_sb[n][:, t, :], MULT)
-        t3 = [sb.tile([P, PACK, VH], F32, name="t3_%d" % half, align_bytes=64) for half in range(2)]
-
-        def third(half, t):
-            nc.vector.tensor_tensor(
-                t3[half][:, t, :],
-                y[t][:].indirect(h_sb[2][:, half * VH // 16 : (half + 1) * VH // 16]),
-                sg_sb[2][:, t, half * VH : (half + 1) * VH],
-                MULT,
-            )
+        t3 = [t12[2][:, :, half * VH : (half + 1) * VH] for half in range(2)]
 
         lo = sb.tile([P, PACK, V], F32, name="lo", align_bytes=64)
         hi = sb.tile([P, PACK, V], F32, name="hi", align_bytes=64)
@@ -138,7 +130,7 @@ def tile_picked_csketch_none_p_kernel(tc, x_words, x_scales, w1, sg1, sg2, sg3, 
         z_f32 = sb.tile([P, PACK, VH], F32, name="z_f32", align_bytes=64)
 
         def clip_above(half):
-            nc.vector.tensor_tensor(mid[half][:], hi[:, :, half * VH : (half + 1) * VH], t3[half][:], MIN)
+            nc.vector.tensor_tensor(mid[half][:], hi[:, :, half * VH : (half + 1) * VH], t3[half], MIN)
 
         def clip_below(half):
             if half == 0:
@@ -193,23 +185,21 @@ def tile_picked_csketch_none_p_kernel(tc, x_words, x_scales, w1, sg1, sg2, sg3, 
                 in_=z_bf[1][:, q * VQ : (q + 1) * VQ, :].rearrange("p v t -> p (v t)"),
             )
 
-        def bounds(half):
+        def bound(dst, op, half):
             cols = slice(half * VH, (half + 1) * VH)
-            nc.vector.tensor_tensor(hi[:, :, cols], t12[0][:, :, cols], t12[1][:, :, cols], MAX)
-            nc.vector.tensor_tensor(lo[:, :, cols], t12[0][:, :, cols], t12[1][:, :, cols], MIN)
+            nc.vector.tensor_tensor(dst[:, :, cols], t12[0][:, :, cols], t12[1][:, :, cols], op)
 
-        for t in range(PACK):
-            third(0, t)
-        bounds(0)
+        bound(hi, MAX, 0)
+        bound(lo, MIN, 0)
         clip_above(0)
+        bound(hi, MAX, 1)
+        clip_below(0)
         for u in range(PACK):
             quantize_w2(u)
-        clip_below(0)
-        bounds(1)
         quantize_z(0)
-        second_product(0, 0, PACK, 7, nc.scalar.copy, nc.sync)
-        for t in range(PACK):
-            third(1, t)
+        second_product(0, 0, 2, 7, nc.scalar.copy, nc.sync)
+        second_product(0, 2, 2, 6, nc.scalar.copy, nc.sync)
+        bound(lo, MIN, 1)
         for step in (clip_above_q, clip_below_q, quantize_z_q):
             for q in range(2):
                 step(q)

@@ -20,7 +20,9 @@ P = 128
 PACK = 4
 W1_VECTOR_ROWS = 48
 VH = V // 2
+VQ = V // 4
 SH = S // 2
+NH = N // 2
 
 
 def tile_picked_csketch_none_p_kernel(tc, x_words, x_scales, w1, sg1, sg2, sg3, w2, offs, h1, h2, h3, out):
@@ -45,9 +47,8 @@ def tile_picked_csketch_none_p_kernel(tc, x_words, x_scales, w1, sg1, sg2, sg3, 
         nc.sync.dma_start(xw[:].bitcast(I32), x_words[0].rearrange("p n t -> p (n t)").bitcast(I32))
         for n, (h, sg) in enumerate(((h1, sg1), (h2, sg2), (h3, sg3))):
             nc.sync.dma_start(h_sb[n][:], h)
-            if n == 1:
-                nc.sync.dma_start(w2_raw[:], w2.rearrange("(p j) c -> p j c", j=PACK))
             nc.sync.dma_start(sg_sb[n][:], sg.rearrange("(p t) v -> p t v", t=PACK))
+        nc.sync.dma_start(w2_raw[:], w2.rearrange("(p j) c -> p j c", j=PACK))
 
         gs = sb.tile([P, S], U8, name="gs", align_bytes=64)
         nc.vector.tensor_copy(gs[:], xs[:].indirect(offs_sb[:]))
@@ -76,76 +77,71 @@ def tile_picked_csketch_none_p_kernel(tc, x_words, x_scales, w1, sg1, sg2, sg3, 
 
         quantize_w1(1)
 
-        def first_product(acc, t, cols):
-            nc.tensor.matmul_mx(
-                out=acc,
-                lhsT=w1_codes[:, t * P : (t + 1) * P].bitcast(FP8X4),
-                lhsT_scale=w1_scales[:, t * P : (t + 1) * P],
-                rhs=gw[:, cols].bitcast(FP8X4),
-                rhs_scale=gs[:, cols],
-                start=True,
-                stop=True,
-            )
-
         y = [sb.tile([P, S], F32, name="y%d" % t, align_bytes=64) for t in range(PACK)]
         pieces = (
             (0, 0, 256, nc.scalar.copy),
             (1, 0, 256, nc.scalar.copy),
-            (0, 256, 384, nc.scalar.copy),
-            (0, 384, 512, nc.vector.tensor_copy),
+            (0, 256, 384, nc.vector.tensor_copy),
+            (0, 384, 512, nc.scalar.copy),
             (1, 256, 512, nc.scalar.copy),
             (2, 0, 512, nc.scalar.copy),
             (3, 0, 512, nc.scalar.copy),
         )
         for n, (t, c0, c1, copy) in enumerate(pieces):
             acc = ps.tile([P, c1 - c0], F32, name="y_ps%d" % n, tag="bank%d" % n)
-            first_product(acc[:], t, slice(c0, c1))
+            nc.tensor.matmul_mx(
+                out=acc[:],
+                lhsT=w1_codes[:, t * P : (t + 1) * P].bitcast(FP8X4),
+                lhsT_scale=w1_scales[:, t * P : (t + 1) * P],
+                rhs=gw[:, c0:c1].bitcast(FP8X4),
+                rhs_scale=gs[:, c0:c1],
+                start=True,
+                stop=True,
+            )
             copy(y[t][:, c0:c1], acc[:])
 
-        w2_bf = [sb.tile([P, P, PACK], BF16, name="w2_bf%d" % u, align_bytes=64) for u in range(PACK)]
-        w2_codes = [sb.tile([P, P], U32, name="w2_codes%d" % u, align_bytes=64) for u in range(PACK)]
-        w2_scales = [sb.tile([P, P], U8, name="w2_scales%d" % u, align_bytes=64) for u in range(PACK)]
-        for u in range(PACK):
-            nc.scalar.copy(
-                w2_bf[u][:],
-                w2_raw[:, :, u * P : (u + 1) * P].rearrange("p j c -> p c j"),
-            )
-
-        def quantize_w2(u):
-            nc.vector.quantize_mx(out=w2_codes[u][:].bitcast(FP8X4), scales=w2_scales[u][:], in_=w2_bf[u][:].rearrange("p m j -> p (m j)"))
-
-        t12 = [sb.tile([P, PACK, V], F32, name="t%d" % n, align_bytes=64) for n in range(3)]
+        tn = [sb.tile([P, PACK, V], F32, name="t%d" % n, align_bytes=64) for n in range(3)]
         for n in range(3):
             for t in range(PACK):
-                nc.vector.tensor_tensor(t12[n][:, t, :], y[t][:].indirect(h_sb[n][:]), sg_sb[n][:, t, :], MULT)
-        t3 = [t12[2][:, :, half * VH : (half + 1) * VH] for half in range(2)]
+                nc.vector.tensor_tensor(tn[n][:, t, :], y[t][:].indirect(h_sb[n][:]), sg_sb[n][:, t, :], MULT)
 
-        lo = sb.tile([P, PACK, V], F32, name="lo", align_bytes=64)
-        hi = sb.tile([P, PACK, V], F32, name="hi", align_bytes=64)
-        mid = [sb.tile([P, PACK, VH], F32, name="mid%d" % half, align_bytes=64) for half in range(2)]
+        w2_bf = [sb.tile([P, NH, PACK], BF16, name="w2_bf%d" % a, tag="shared%d" % a, align_bytes=64) for a in range(2)]
+        w2_codes = sb.tile([P, N], U32, name="w2_codes", align_bytes=64)
+        w2_scales = sb.tile([P, N], U8, name="w2_scales", align_bytes=64)
+        for a in range(2):
+            cols = slice(a * NH, (a + 1) * NH)
+            nc.scalar.copy(w2_bf[a][:], w2_raw[:, :, cols].rearrange("p j c -> p c j"))
+            nc.vector.quantize_mx(out=w2_codes[:, cols].bitcast(FP8X4), scales=w2_scales[:, cols], in_=w2_bf[a][:].rearrange("p c j -> p (c j)"))
+
+        late = sb.tile([P, 3, PACK, VH], F32, name="late", tag="shared1", align_bytes=64)
+        hi = [sb.tile([P, PACK, VH], F32, name="hi0", tag="shared0", align_bytes=64)[:], late[:, 0]]
+        lo = [late[:, 1], late[:, 2]]
+        mid = [sb.tile([P, PACK, VH], F32, name="mid%d" % half, align_bytes=64)[:] for half in range(2)]
         z_bf = [sb.tile([P, VH, PACK], BF16, name="z_bf%d" % half, align_bytes=64) for half in range(2)]
         z_codes = [sb.tile([P, VH], U32, name="z_codes%d" % half, align_bytes=64) for half in range(2)]
         z_scales = [sb.tile([P, VH], U8, name="z_scales%d" % half, align_bytes=64) for half in range(2)]
 
-        z_f32 = sb.tile([P, PACK, VH], F32, name="z_f32", align_bytes=64)
+        def bound(dst, op, half):
+            cols = slice(half * VH, (half + 1) * VH)
+            nc.vector.tensor_tensor(dst[half], tn[0][:, :, cols], tn[1][:, :, cols], op)
 
-        def clip_above(half):
-            nc.vector.tensor_tensor(mid[half][:], hi[:, :, half * VH : (half + 1) * VH], t3[half], MIN)
+        def clip_above(half, c0, c1):
+            nc.vector.tensor_tensor(mid[half][:, :, c0:c1], hi[half][:, :, c0:c1], tn[2][:, :, half * VH + c0 : half * VH + c1], MIN)
 
-        def clip_below(half):
-            if half == 0:
-                nc.vector.tensor_tensor(z_f32[:], lo[:, :, :VH], mid[0][:], MAX)
-                nc.scalar.copy(z_bf[0][:], z_f32[:].rearrange("p t v -> p v t"))
-            else:
-                nc.vector.tensor_tensor(
-                    z_bf[1][:],
-                    lo[:, :, VH:].rearrange("p t v -> p v t"),
-                    mid[1][:].rearrange("p t v -> p v t"),
-                    MAX,
-                )
+        def clip_below(half, c0, c1):
+            nc.vector.tensor_tensor(
+                z_bf[half][:, c0:c1, :],
+                lo[half][:, :, c0:c1].rearrange("p t v -> p v t"),
+                mid[half][:, :, c0:c1].rearrange("p t v -> p v t"),
+                MAX,
+            )
 
-        def quantize_z(half):
-            nc.vector.quantize_mx(out=z_codes[half][:].bitcast(FP8X4), scales=z_scales[half][:], in_=z_bf[half][:].rearrange("p v t -> p (v t)"))
+        def quantize_z(half, c0, c1):
+            nc.vector.quantize_mx(
+                out=z_codes[half][:, c0:c1].bitcast(FP8X4),
+                scales=z_scales[half][:, c0:c1],
+                in_=z_bf[half][:, c0:c1, :].rearrange("p v t -> p (v t)"),
+            )
 
         out_rows = out.rearrange("(u p) v -> p u v", p=P)
 
@@ -154,8 +150,8 @@ def tile_picked_csketch_none_p_kernel(tc, x_words, x_scales, w1, sg1, sg2, sg3, 
             for u in range(u0, u0 + count):
                 nc.tensor.matmul_mx(
                     out=acc[:, u - u0, :],
-                    lhsT=w2_codes[u][:].bitcast(FP8X4),
-                    lhsT_scale=w2_scales[u][:],
+                    lhsT=w2_codes[:, u * P : (u + 1) * P].bitcast(FP8X4),
+                    lhsT_scale=w2_scales[:, u * P : (u + 1) * P],
                     rhs=z_codes[half][:].bitcast(FP8X4),
                     rhs_scale=z_scales[half][:],
                     start=True,
@@ -165,44 +161,18 @@ def tile_picked_csketch_none_p_kernel(tc, x_words, x_scales, w1, sg1, sg2, sg3, 
             copy_engine(res[:], acc[:])
             store_engine.dma_start(out_rows[:, u0 : u0 + count, half * VH : (half + 1) * VH], res[:])
 
-        VQ = VH // 2
-
-        def clip_above_q(q):
-            nc.vector.tensor_tensor(mid[1][:, :, q * VQ : (q + 1) * VQ], hi[:, :, VH + q * VQ : VH + (q + 1) * VQ], t3[1][:, :, q * VQ : (q + 1) * VQ], MIN)
-
-        def clip_below_q(q):
-            nc.vector.tensor_tensor(
-                z_bf[1][:, q * VQ : (q + 1) * VQ, :],
-                lo[:, :, VH + q * VQ : VH + (q + 1) * VQ].rearrange("p t v -> p v t"),
-                mid[1][:, :, q * VQ : (q + 1) * VQ].rearrange("p t v -> p v t"),
-                MAX,
-            )
-
-        def quantize_z_q(q):
-            nc.vector.quantize_mx(
-                out=z_codes[1][:, q * VQ : (q + 1) * VQ].bitcast(FP8X4),
-                scales=z_scales[1][:, q * VQ : (q + 1) * VQ],
-                in_=z_bf[1][:, q * VQ : (q + 1) * VQ, :].rearrange("p v t -> p (v t)"),
-            )
-
-        def bound(dst, op, half):
-            cols = slice(half * VH, (half + 1) * VH)
-            nc.vector.tensor_tensor(dst[:, :, cols], t12[0][:, :, cols], t12[1][:, :, cols], op)
-
         bound(hi, MAX, 0)
         bound(lo, MIN, 0)
-        clip_above(0)
+        clip_above(0, 0, VH)
         bound(hi, MAX, 1)
-        clip_below(0)
-        for u in range(PACK):
-            quantize_w2(u)
-        quantize_z(0)
+        clip_below(0, 0, VH)
+        bound(lo, MIN, 1)
+        quantize_z(0, 0, VH)
         second_product(0, 0, 2, 7, nc.scalar.copy, nc.sync)
         second_product(0, 2, 2, 6, nc.scalar.copy, nc.sync)
-        bound(lo, MIN, 1)
-        for step in (clip_above_q, clip_below_q, quantize_z_q):
+        for step in (clip_above, clip_below, quantize_z):
             for q in range(2):
-                step(q)
+                step(1, q * VQ, (q + 1) * VQ)
         for u in range(PACK):
             if u % 2 == 0:
                 second_product(1, u, 1, u, nc.scalar.copy, nc.scalar)

@@ -47,8 +47,9 @@ def tile_picked_csketch_none_p_kernel(tc, x_words, x_scales, w1, sg1, sg2, sg3, 
         nc.sync.dma_start(xw[:].bitcast(I32), x_words[0].rearrange("p n t -> p (n t)").bitcast(I32))
         for n, (h, sg) in enumerate(((h1, sg1), (h2, sg2), (h3, sg3))):
             nc.sync.dma_start(h_sb[n][:], h)
+            if n == 2:
+                nc.sync.dma_start(w2_raw[:], w2.rearrange("(p j) c -> p j c", j=PACK))
             nc.sync.dma_start(sg_sb[n][:], sg.rearrange("(p t) v -> p t v", t=PACK))
-        nc.sync.dma_start(w2_raw[:], w2.rearrange("(p j) c -> p j c", j=PACK))
 
         gs = sb.tile([P, S], U8, name="gs", align_bytes=64)
         nc.vector.tensor_copy(gs[:], xs[:].indirect(offs_sb[:]))
@@ -77,7 +78,7 @@ def tile_picked_csketch_none_p_kernel(tc, x_words, x_scales, w1, sg1, sg2, sg3, 
 
         quantize_w1(1)
 
-        y = [sb.tile([P, S], F32, name="y%d" % t, align_bytes=64) for t in range(PACK)]
+        y = [sb.tile([P, S], F32, name="y%d" % t, tag="y%d" % t, align_bytes=64) for t in range(PACK)]
         pieces = (
             (0, 0, 256, nc.scalar.copy),
             (1, 0, 256, nc.scalar.copy),
@@ -105,7 +106,7 @@ def tile_picked_csketch_none_p_kernel(tc, x_words, x_scales, w1, sg1, sg2, sg3, 
             for t in range(PACK):
                 nc.vector.tensor_tensor(tn[n][:, t, :], y[t][:].indirect(h_sb[n][:]), sg_sb[n][:, t, :], MULT)
 
-        w2_bf = [sb.tile([P, NH, PACK], BF16, name="w2_bf%d" % a, tag="shared%d" % a, align_bytes=64) for a in range(2)]
+        w2_bf = [sb.tile([P, NH, PACK], BF16, name="w2_bf%d" % a, align_bytes=64) for a in range(2)]
         w2_codes = sb.tile([P, N], U32, name="w2_codes", align_bytes=64)
         w2_scales = sb.tile([P, N], U8, name="w2_scales", align_bytes=64)
         for a in range(2):
@@ -113,17 +114,16 @@ def tile_picked_csketch_none_p_kernel(tc, x_words, x_scales, w1, sg1, sg2, sg3, 
             nc.scalar.copy(w2_bf[a][:], w2_raw[:, :, cols].rearrange("p j c -> p c j"))
             nc.vector.quantize_mx(out=w2_codes[:, cols].bitcast(FP8X4), scales=w2_scales[:, cols], in_=w2_bf[a][:].rearrange("p c j -> p (c j)"))
 
-        late = sb.tile([P, 3, PACK, VH], F32, name="late", tag="shared1", align_bytes=64)
-        hi = [sb.tile([P, PACK, VH], F32, name="hi0", tag="shared0", align_bytes=64)[:], late[:, 0]]
-        lo = [late[:, 1], late[:, 2]]
+        hi = [sb.tile([P, PACK, VH], F32, name="hi%d" % half, tag="y%d" % (2 * half), align_bytes=64)[:] for half in range(2)]
+        lo = [sb.tile([P, PACK, VH], F32, name="lo%d" % half, tag="y%d" % (2 * half + 1), align_bytes=64)[:] for half in range(2)]
         mid = [sb.tile([P, PACK, VH], F32, name="mid%d" % half, align_bytes=64)[:] for half in range(2)]
         z_bf = [sb.tile([P, VH, PACK], BF16, name="z_bf%d" % half, align_bytes=64) for half in range(2)]
         z_codes = [sb.tile([P, VH], U32, name="z_codes%d" % half, align_bytes=64) for half in range(2)]
         z_scales = [sb.tile([P, VH], U8, name="z_scales%d" % half, align_bytes=64) for half in range(2)]
 
-        def bound(dst, op, half):
-            cols = slice(half * VH, (half + 1) * VH)
-            nc.vector.tensor_tensor(dst[half], tn[0][:, :, cols], tn[1][:, :, cols], op)
+        def bound(dst, op, half, c0, c1):
+            cols = slice(half * VH + c0, half * VH + c1)
+            nc.vector.tensor_tensor(dst[half][:, :, c0:c1], tn[0][:, :, cols], tn[1][:, :, cols], op)
 
         def clip_above(half, c0, c1):
             nc.vector.tensor_tensor(mid[half][:, :, c0:c1], hi[half][:, :, c0:c1], tn[2][:, :, half * VH + c0 : half * VH + c1], MIN)
@@ -161,16 +161,19 @@ def tile_picked_csketch_none_p_kernel(tc, x_words, x_scales, w1, sg1, sg2, sg3, 
             copy_engine(res[:], acc[:])
             store_engine.dma_start(out_rows[:, u0 : u0 + count, half * VH : (half + 1) * VH], res[:])
 
-        bound(hi, MAX, 0)
-        bound(lo, MIN, 0)
+        bound(hi, MAX, 0, 0, VH)
+        bound(lo, MIN, 0, 0, VH)
         clip_above(0, 0, VH)
-        bound(hi, MAX, 1)
+        bound(hi, MAX, 1, 0, VQ)
         clip_below(0, 0, VH)
-        bound(lo, MIN, 1)
+        bound(hi, MAX, 1, VQ, VH)
         quantize_z(0, 0, VH)
         second_product(0, 0, 2, 7, nc.scalar.copy, nc.sync)
         second_product(0, 2, 2, 6, nc.scalar.copy, nc.sync)
-        for step in (clip_above, clip_below, quantize_z):
+        clip_above(1, 0, VH)
+        bound(lo, MIN, 1, 0, VQ)
+        bound(lo, MIN, 1, VQ, VH)
+        for step in (clip_below, quantize_z):
             for q in range(2):
                 step(1, q * VQ, (q + 1) * VQ)
         for u in range(PACK):

@@ -36,8 +36,8 @@ def tile_picked_csketch_none_p_kernel(tc, x_words, x_scales, w1, sg1, sg2, sg3, 
         xw = sb.tile([P, T], U32, name="xw", align_bytes=64)
         xs = sb.tile([P, T], U8, name="xs", align_bytes=64)
         w1_raw = sb.tile([P, PACK, H], F32, name="w1_raw", align_bytes=64)
-        w2_raw = sb.tile([P, PACK, N], F32, name="w2_raw", align_bytes=64)
-        sg_sb = [sb.tile([P, PACK, V], F32, name="sg%d_sb" % n, align_bytes=64) for n in range(3)]
+        w2_raw = sb.tile([P, PACK, N], F32, name="w2_raw", tag="w2_raw", align_bytes=64)
+        sg_sb = [sb.tile([P, PACK, V], F32, name="sg%d_sb" % n, tag="sg%d" % n, align_bytes=64) for n in range(3)]
 
         nc.vector.memset(xs[:].bitcast(I32), 0)
         nc.sync.dma_start(w1_raw[:], w1.rearrange("(p j) c -> p j c", j=PACK))
@@ -107,34 +107,29 @@ def tile_picked_csketch_none_p_kernel(tc, x_words, x_scales, w1, sg1, sg2, sg3, 
                 nc.vector.tensor_tensor(tn[n][:, t, :], y[t][:].indirect(h_sb[n][:]), sg_sb[n][:, t, :], MULT)
 
         w2_bf = [sb.tile([P, NH, PACK], BF16, name="w2_bf%d" % a, align_bytes=64) for a in range(2)]
-        w2_codes = sb.tile([P, N], U32, name="w2_codes", align_bytes=64)
-        w2_scales = sb.tile([P, N], U8, name="w2_scales", align_bytes=64)
         for a in range(2):
+            nc.scalar.copy(w2_bf[a][:], w2_raw[:, :, a * NH : (a + 1) * NH].rearrange("p j c -> p c j"))
+        w2_codes = sb.tile([P, N], U32, name="w2_codes", tag="sg2", align_bytes=64)
+        w2_scales = sb.tile([P, N], U8, name="w2_scales", align_bytes=64)
+
+        def quantize_w2(a):
             cols = slice(a * NH, (a + 1) * NH)
-            nc.scalar.copy(w2_bf[a][:], w2_raw[:, :, cols].rearrange("p j c -> p c j"))
             nc.vector.quantize_mx(out=w2_codes[:, cols].bitcast(FP8X4), scales=w2_scales[:, cols], in_=w2_bf[a][:].rearrange("p c j -> p (c j)"))
 
-        hi = [sb.tile([P, PACK, VH], F32, name="hi%d" % half, tag="y%d" % (2 * half), align_bytes=64)[:] for half in range(2)]
-        lo = [sb.tile([P, PACK, VH], F32, name="lo%d" % half, tag="y%d" % (2 * half + 1), align_bytes=64)[:] for half in range(2)]
-        mid = [sb.tile([P, PACK, VH], F32, name="mid%d" % half, align_bytes=64)[:] for half in range(2)]
+        woven = sb.tile([P, 3, VH, PACK], F32, name="woven", tag="w2_raw", align_bytes=64)
+        for n in range(3):
+            nc.scalar.copy(woven[:, n], tn[n][:, :, VH:].rearrange("p t v -> p v t"))
+
+        hi0 = sb.tile([P, PACK, VH], F32, name="hi0", tag="y0", align_bytes=64)
+        lo0 = sb.tile([P, PACK, VH], F32, name="lo0", tag="y1", align_bytes=64)
+        mid0 = sb.tile([P, PACK, VH], F32, name="mid0", align_bytes=64)
+        z0 = sb.tile([P, PACK, VH], F32, name="z0", align_bytes=64)
+        hi1 = sb.tile([P, VH, PACK], F32, name="hi1", tag="y2", align_bytes=64)
+        lo1 = sb.tile([P, VH, PACK], F32, name="lo1", tag="y3", align_bytes=64)
+        mid1 = sb.tile([P, VH, PACK], F32, name="mid1", align_bytes=64)
         z_bf = [sb.tile([P, VH, PACK], BF16, name="z_bf%d" % half, align_bytes=64) for half in range(2)]
         z_codes = [sb.tile([P, VH], U32, name="z_codes%d" % half, align_bytes=64) for half in range(2)]
         z_scales = [sb.tile([P, VH], U8, name="z_scales%d" % half, align_bytes=64) for half in range(2)]
-
-        def bound(dst, op, half, c0, c1):
-            cols = slice(half * VH + c0, half * VH + c1)
-            nc.vector.tensor_tensor(dst[half][:, :, c0:c1], tn[0][:, :, cols], tn[1][:, :, cols], op)
-
-        def clip_above(half, c0, c1):
-            nc.vector.tensor_tensor(mid[half][:, :, c0:c1], hi[half][:, :, c0:c1], tn[2][:, :, half * VH + c0 : half * VH + c1], MIN)
-
-        def clip_below(half, c0, c1):
-            nc.vector.tensor_tensor(
-                z_bf[half][:, c0:c1, :],
-                lo[half][:, :, c0:c1].rearrange("p t v -> p v t"),
-                mid[half][:, :, c0:c1].rearrange("p t v -> p v t"),
-                MAX,
-            )
 
         def quantize_z(half, c0, c1):
             nc.vector.quantize_mx(
@@ -161,21 +156,25 @@ def tile_picked_csketch_none_p_kernel(tc, x_words, x_scales, w1, sg1, sg2, sg3, 
             copy_engine(res[:], acc[:])
             store_engine.dma_start(out_rows[:, u0 : u0 + count, half * VH : (half + 1) * VH], res[:])
 
-        bound(hi, MAX, 0, 0, VH)
-        bound(lo, MIN, 0, 0, VH)
-        clip_above(0, 0, VH)
-        bound(hi, MAX, 1, 0, VQ)
-        clip_below(0, 0, VH)
-        bound(hi, MAX, 1, VQ, VH)
+        nc.vector.tensor_tensor(hi0[:], tn[0][:, :, :VH], tn[1][:, :, :VH], MAX)
+        nc.vector.tensor_tensor(lo0[:], tn[0][:, :, :VH], tn[1][:, :, :VH], MIN)
+        nc.vector.tensor_tensor(mid0[:], hi0[:], tn[2][:, :, :VH], MIN)
+        quantize_w2(0)
+        nc.vector.tensor_tensor(z0[:], lo0[:], mid0[:], MAX)
+        nc.scalar.copy(z_bf[0][:], z0[:].rearrange("p t v -> p v t"))
+        quantize_w2(1)
         quantize_z(0, 0, VH)
         second_product(0, 0, 2, 7, nc.scalar.copy, nc.sync)
         second_product(0, 2, 2, 6, nc.scalar.copy, nc.sync)
-        clip_above(1, 0, VH)
-        bound(lo, MIN, 1, 0, VQ)
-        bound(lo, MIN, 1, VQ, VH)
-        for step in (clip_below, quantize_z):
-            for q in range(2):
-                step(1, q * VQ, (q + 1) * VQ)
+        nc.vector.tensor_tensor(hi1[:], woven[:, 0], woven[:, 1], MAX)
+        nc.vector.tensor_tensor(lo1[:], woven[:, 0], woven[:, 1], MIN)
+        quarters = [slice(q * VQ, (q + 1) * VQ) for q in range(2)]
+        for keys in quarters:
+            nc.vector.tensor_tensor(mid1[:, keys], hi1[:, keys], woven[:, 2, keys], MIN)
+        for keys in quarters:
+            nc.vector.tensor_tensor(z_bf[1][:, keys], lo1[:, keys], mid1[:, keys], MAX)
+        for keys in quarters:
+            quantize_z(1, keys.start, keys.stop)
         for u in range(PACK):
             if u % 2 == 0:
                 second_product(1, u, 1, u, nc.scalar.copy, nc.scalar)

@@ -18,6 +18,7 @@ MAX = mybir.AluOpType.max
 
 P = 128
 PACK = 4
+LINE = 4
 W1_VECTOR_ROWS = 48
 VH = V // 2
 VQ = V // 4
@@ -55,8 +56,8 @@ def tile_picked_csketch_none_p_kernel(tc, x_words, x_scales, w1, sg1, sg2, sg3, 
         nc.vector.tensor_copy(gs[:], xs[:].indirect(offs_sb[:]))
 
         w1_bf = sb.tile([P, PACK, P, PACK], BF16, name="w1_bf", align_bytes=64)
-        src = w1_raw[:].rearrange("p j (m t) -> p m t j", t=PACK)
-        dst = w1_bf[:].rearrange("p t m j -> p m t j")
+        src = w1_raw[:].rearrange("p j (m t) -> p m j t", t=PACK)
+        dst = w1_bf[:].rearrange("p t m j -> p m j t")
         nc.vector.tensor_copy(dst[:, :W1_VECTOR_ROWS], src[:, :W1_VECTOR_ROWS])
         nc.scalar.copy(dst[:, W1_VECTOR_ROWS:], src[:, W1_VECTOR_ROWS:])
         w1_codes = sb.tile([P, H], U32, name="w1_codes", align_bytes=64)
@@ -107,8 +108,12 @@ def tile_picked_csketch_none_p_kernel(tc, x_words, x_scales, w1, sg1, sg2, sg3, 
                 nc.vector.tensor_tensor(tn[n][:, t, :], y[t][:].indirect(h_sb[n][:]), sg_sb[n][:, t, :], MULT)
 
         w2_bf = [sb.tile([P, NH, PACK], BF16, name="w2_bf%d" % a, align_bytes=64) for a in range(2)]
+
+        def interleave(dst, planes):
+            nc.scalar.copy(dst.rearrange("p (c i) t -> p c t i", i=LINE), planes.rearrange("p t (c i) -> p c t i", i=LINE))
+
         for a in range(2):
-            nc.scalar.copy(w2_bf[a][:], w2_raw[:, :, a * NH : (a + 1) * NH].rearrange("p j c -> p c j"))
+            interleave(w2_bf[a][:], w2_raw[:, :, a * NH : (a + 1) * NH])
         w2_codes = sb.tile([P, N], U32, name="w2_codes", tag="sg2", align_bytes=64)
         w2_scales = sb.tile([P, N], U8, name="w2_scales", align_bytes=64)
 
@@ -118,7 +123,7 @@ def tile_picked_csketch_none_p_kernel(tc, x_words, x_scales, w1, sg1, sg2, sg3, 
 
         woven = sb.tile([P, 3, VH, PACK], F32, name="woven", tag="w2_raw", align_bytes=64)
         for n in range(3):
-            nc.scalar.copy(woven[:, n], tn[n][:, :, VH:].rearrange("p t v -> p v t"))
+            interleave(woven[:, n], tn[n][:, :, VH:])
 
         hi0 = sb.tile([P, PACK, VH], F32, name="hi0", tag="y0", align_bytes=64)
         lo0 = sb.tile([P, PACK, VH], F32, name="lo0", tag="y1", align_bytes=64)
@@ -161,7 +166,7 @@ def tile_picked_csketch_none_p_kernel(tc, x_words, x_scales, w1, sg1, sg2, sg3, 
         nc.vector.tensor_tensor(mid0[:], hi0[:], tn[2][:, :, :VH], MIN)
         quantize_w2(0)
         nc.vector.tensor_tensor(z0[:], lo0[:], mid0[:], MAX)
-        nc.scalar.copy(z_bf[0][:], z0[:].rearrange("p t v -> p v t"))
+        interleave(z_bf[0][:], z0[:])
         quantize_w2(1)
         quantize_z(0, 0, VH)
         second_product(0, 0, 2, 7, nc.scalar.copy, nc.sync)

@@ -1,6 +1,7 @@
 from contextlib import ExitStack
 
 import concourse.mybir as mybir
+from concourse.masks import make_identity
 
 K, T, S, V, N, H = 512, 2048, 512, 256, 512, 512
 FLOPS = 2 * K * H * S + 2 * H * N * V
@@ -15,6 +16,8 @@ FP8X4 = mybir.dt.float8_e4m3fn_x4
 MULT = mybir.AluOpType.mult
 MIN = mybir.AluOpType.min
 MAX = mybir.AluOpType.max
+COPY = mybir.ActivationFunctionType.Copy
+RELU = mybir.ActivationFunctionType.Relu
 
 P = 128
 PACK = 4
@@ -40,6 +43,10 @@ def tile_picked_csketch_none_p_kernel(tc, x_words, x_scales, w1, sg1, sg2, sg3, 
         w2_raw = sb.tile([P, PACK, N], F32, name="w2_raw", tag="w2_raw", align_bytes=64)
         sg_sb = [sb.tile([P, PACK, V], F32, name="sg%d_sb" % n, tag="sg%d" % n, align_bytes=64) for n in range(3)]
 
+        ident = sb.tile([P, P], F32, name="ident", align_bytes=64)
+        make_identity(nc, ident[:])
+        minus_one = sb.tile([P, 1], F32, name="minus_one", tag="a_turned", align_bytes=64)
+        nc.gpsimd.memset(minus_one[:], -1.0)
         nc.vector.memset(xs[:].bitcast(I32), 0)
         nc.sync.dma_start(w1_raw[:], w1.rearrange("(p j) c -> p j c", j=PACK))
         nc.sync.dma_start(offs_sb[:], offs)
@@ -102,11 +109,31 @@ def tile_picked_csketch_none_p_kernel(tc, x_words, x_scales, w1, sg1, sg2, sg3, 
             )
             copy(y[t][:, c0:c1], acc[:])
 
+        nc.scalar.activation(sg_sb[1][:, :, VH:], sg_sb[1][:, :, VH:], COPY, scale=minus_one[:])
+
         tn = [sb.tile([P, PACK, V], F32, name="t%d" % n, align_bytes=64) for n in range(3)]
-        for n in range(3):
+
+        def look_up(n):
             for t in range(PACK):
                 nc.vector.tensor_tensor(tn[n][:, t, :], y[t][:].indirect(h_sb[n][:]), sg_sb[n][:, t, :], MULT)
 
+        def turn(acc, src, start, stop):
+            for t in range(PACK):
+                nc.tensor.matmul(acc[:, t, :], src[:, t, :], ident[:], start=start and t == 0, stop=stop and t == PACK - 1, is_transpose=True)
+
+        look_up(0)
+        a_ps = ps.tile([P, PACK, P], F32, name="a_ps", tag="bank7")
+        diff_ps = ps.tile([P, PACK, P], F32, name="diff_ps", tag="bank0")
+        turn(a_ps, tn[0][:, :, VH:], True, True)
+        turn(diff_ps, tn[0][:, :, VH:], True, False)
+        a_turned = sb.tile([P, PACK, P], F32, name="a_turned", tag="a_turned", align_bytes=64)
+        nc.scalar.copy(a_turned[:], a_ps[:])
+        hi_ps = ps.tile([P, PACK, VH], F32, name="hi_ps", tag="bank3")
+        turn(hi_ps, a_turned, True, False)
+        look_up(1)
+        b_ps = ps.tile([P, PACK, P], F32, name="b_ps", tag="bank2")
+        turn(diff_ps, tn[1][:, :, VH:], False, True)
+        turn(b_ps, tn[1][:, :, VH:], True, True)
         w2_bf = [sb.tile([P, NH, PACK], BF16, name="w2_bf%d" % a, align_bytes=64) for a in range(2)]
 
         def interleave(dst, planes):
@@ -114,27 +141,40 @@ def tile_picked_csketch_none_p_kernel(tc, x_words, x_scales, w1, sg1, sg2, sg3, 
 
         for a in range(2):
             interleave(w2_bf[a][:], w2_raw[:, :, a * NH : (a + 1) * NH])
-        w2_codes = sb.tile([P, N], U32, name="w2_codes", tag="sg2", align_bytes=64)
+        turned = sb.tile([P, 2, PACK, P], F32, name="turned", tag="w2_raw", align_bytes=64)
+        gap = turned[:, 0]
+        b_turned = turned[:, 1]
+        nc.scalar.activation(gap, diff_ps[:], RELU, scale=-1.0)
+        nc.scalar.copy(b_turned, b_ps[:])
+        turn(hi_ps, gap, False, True)
+        nlo_ps = ps.tile([P, PACK, VH], F32, name="nlo_ps", tag="bank1")
+        turn(nlo_ps, gap, True, False)
+        turn(nlo_ps, b_turned, False, True)
+        look_up(2)
+
+        w2_codes = []
         w2_scales = sb.tile([P, N], U8, name="w2_scales", align_bytes=64)
 
         def quantize_w2(a):
             cols = slice(a * NH, (a + 1) * NH)
-            nc.vector.quantize_mx(out=w2_codes[:, cols].bitcast(FP8X4), scales=w2_scales[:, cols], in_=w2_bf[a][:].rearrange("p c j -> p (c j)"))
-
-        woven = sb.tile([P, 3, VH, PACK], F32, name="woven", tag="w2_raw", align_bytes=64)
-        for n in range(3):
-            interleave(woven[:, n], tn[n][:, :, VH:])
+            if a == 0:
+                both = sb.tile([P, 2, NH], U32, name="w2_codes", tag="y0", align_bytes=64)
+                w2_codes.extend([both[:, 0], both[:, 1]])
+            nc.vector.quantize_mx(out=w2_codes[a].bitcast(FP8X4), scales=w2_scales[:, cols], in_=w2_bf[a][:].rearrange("p c j -> p (c j)"))
 
         hi0 = sb.tile([P, PACK, VH], F32, name="hi0", tag="y0", align_bytes=64)
         lo0 = sb.tile([P, PACK, VH], F32, name="lo0", tag="y1", align_bytes=64)
-        mid0 = sb.tile([P, PACK, VH], F32, name="mid0", align_bytes=64)
+        mid0 = sb.tile([P, PACK, VH], F32, name="mid0", tag="mid0", align_bytes=64)
         z0 = sb.tile([P, PACK, VH], F32, name="z0", align_bytes=64)
-        hi1 = sb.tile([P, VH, PACK], F32, name="hi1", tag="y2", align_bytes=64)
-        lo1 = sb.tile([P, VH, PACK], F32, name="lo1", tag="y3", align_bytes=64)
+        woven = sb.tile([P, VH, PACK], F32, name="woven", align_bytes=64)
         mid1 = sb.tile([P, VH, PACK], F32, name="mid1", align_bytes=64)
-        z_bf = [sb.tile([P, VH, PACK], BF16, name="z_bf%d" % half, align_bytes=64) for half in range(2)]
+        interleave(woven[:], tn[2][:, :, VH:])
+        z_bf = [sb.tile([P, VH, PACK], BF16, name="z_bf%d" % half, tag="z_bf%d" % half, align_bytes=64) for half in range(2)]
         z_codes = [sb.tile([P, VH], U32, name="z_codes%d" % half, align_bytes=64) for half in range(2)]
         z_scales = [sb.tile([P, VH], U8, name="z_scales%d" % half, align_bytes=64) for half in range(2)]
+
+        def clip_above(keys):
+            nc.vector.tensor_tensor(mid1[:, keys], hi_ps[:, :, keys].rearrange("p t v -> p v t"), woven[:, keys], MIN)
 
         def quantize_z(half, c0, c1):
             nc.vector.quantize_mx(
@@ -150,7 +190,7 @@ def tile_picked_csketch_none_p_kernel(tc, x_words, x_scales, w1, sg1, sg2, sg3, 
             for u in range(u0, u0 + count):
                 nc.tensor.matmul_mx(
                     out=acc[:, u - u0, :],
-                    lhsT=w2_codes[:, u * P : (u + 1) * P].bitcast(FP8X4),
+                    lhsT=w2_codes[u // 2][:, u % 2 * P : (u % 2 + 1) * P].bitcast(FP8X4),
                     lhsT_scale=w2_scales[:, u * P : (u + 1) * P],
                     rhs=z_codes[half][:].bitcast(FP8X4),
                     rhs_scale=z_scales[half][:],
@@ -163,25 +203,23 @@ def tile_picked_csketch_none_p_kernel(tc, x_words, x_scales, w1, sg1, sg2, sg3, 
 
         nc.vector.tensor_tensor(hi0[:], tn[0][:, :, :VH], tn[1][:, :, :VH], MAX)
         nc.vector.tensor_tensor(lo0[:], tn[0][:, :, :VH], tn[1][:, :, :VH], MIN)
-        nc.vector.tensor_tensor(mid0[:], hi0[:], tn[2][:, :, :VH], MIN)
-        quantize_w2(0)
+        nc.vector.tensor_tensor(mid0[:], tn[2][:, :, :VH], hi0[:], MIN)
+        quarters = [slice(q * VQ, (q + 1) * VQ) for q in range(2)]
+        clip_above(quarters[0])
         nc.vector.tensor_tensor(z0[:], lo0[:], mid0[:], MAX)
         interleave(z_bf[0][:], z0[:])
+        quantize_w2(0)
         quantize_w2(1)
         quantize_z(0, 0, VH)
         second_product(0, 0, 2, 7, nc.scalar.copy, nc.sync)
-        second_product(0, 2, 2, 6, nc.scalar.copy, nc.sync)
-        nc.vector.tensor_tensor(hi1[:], woven[:, 0], woven[:, 1], MAX)
-        nc.vector.tensor_tensor(lo1[:], woven[:, 0], woven[:, 1], MIN)
-        quarters = [slice(q * VQ, (q + 1) * VQ) for q in range(2)]
+        second_product(0, 2, 2, 2, nc.scalar.copy, nc.sync)
+        clip_above(quarters[1])
         for keys in quarters:
-            nc.vector.tensor_tensor(mid1[:, keys], hi1[:, keys], woven[:, 2, keys], MIN)
-        for keys in quarters:
-            nc.vector.tensor_tensor(z_bf[1][:, keys], lo1[:, keys], mid1[:, keys], MAX)
+            nc.vector.scalar_tensor_tensor(z_bf[1][:, keys], nlo_ps[:, :, keys].rearrange("p t v -> p v t"), -1.0, mid1[:, keys], MULT, MAX)
         for keys in quarters:
             quantize_z(1, keys.start, keys.stop)
         for u in range(PACK):
             if u % 2 == 0:
-                second_product(1, u, 1, u, nc.scalar.copy, nc.scalar)
+                second_product(1, u, 1, (4, 5, 6, 0)[u], nc.scalar.copy, nc.scalar)
             else:
-                second_product(1, u, 1, u, nc.vector.tensor_copy, nc.sync)
+                second_product(1, u, 1, (4, 5, 6, 0)[u], nc.vector.tensor_copy, nc.sync)

@@ -33,6 +33,7 @@ def tile_picked_csketch_none_p_kernel(tc, x_words, x_scales, w1, sg1, sg2, sg3, 
     nc = tc.nc
     with ExitStack() as ctx:
         sb = ctx.enter_context(tc.tile_pool(name="sb", bufs=1))
+        yp = ctx.enter_context(tc.tile_pool(name="yp", bufs=1))
         ps = ctx.enter_context(tc.psum_pool(name="ps", bufs=1))
 
         offs_sb = sb.tile([P, S // 16], U16, name="offs_sb")
@@ -45,8 +46,9 @@ def tile_picked_csketch_none_p_kernel(tc, x_words, x_scales, w1, sg1, sg2, sg3, 
 
         ident = sb.tile([P, P], F32, name="ident", align_bytes=64)
         make_identity(nc, ident[:])
-        minus_one = sb.tile([P, 1], F32, name="minus_one", tag="a_turned", align_bytes=64)
-        nc.gpsimd.memset(minus_one[:], -1.0)
+        y_room = yp.tile([P, PACK * S], F32, name="y_room", offset=0, align_bytes=64)
+        minus_one = y_room[:, 0:1]
+        nc.gpsimd.memset(minus_one, -1.0)
         nc.vector.memset(xs[:].bitcast(I32), 0)
         nc.sync.dma_start(w1_raw[:], w1.rearrange("(p j) c -> p j c", j=PACK))
         nc.sync.dma_start(offs_sb[:], offs)
@@ -54,10 +56,16 @@ def tile_picked_csketch_none_p_kernel(tc, x_words, x_scales, w1, sg1, sg2, sg3, 
             nc.sync.dma_start(xs[q:P:32, :].bitcast(I32), x_scales[0, q:16:4, :].bitcast(I32))
         nc.sync.dma_start(xw[:].bitcast(I32), x_words[0].rearrange("p n t -> p (n t)").bitcast(I32))
         for n, (h, sg) in enumerate(((h1, sg1), (h2, sg2), (h3, sg3))):
+            planes = sg.rearrange("(p t) v -> p t v", t=PACK)
+            if n == 0:
+                nc.sync.dma_start(sg_sb[n][:, :, VH:], planes[:, :, VH:])
+                nc.sync.dma_start(h_sb[n][:], h)
+                nc.sync.dma_start(sg_sb[n][:, :, :VH], planes[:, :, :VH])
+                continue
             nc.sync.dma_start(h_sb[n][:], h)
             if n == 2:
                 nc.sync.dma_start(w2_raw[:], w2.rearrange("(p j) c -> p j c", j=PACK))
-            nc.sync.dma_start(sg_sb[n][:], sg.rearrange("(p t) v -> p t v", t=PACK))
+            nc.sync.dma_start(sg_sb[n][:], planes)
 
         gs = sb.tile([P, S], U8, name="gs", align_bytes=64)
         nc.vector.tensor_copy(gs[:], xs[:].indirect(offs_sb[:]))
@@ -85,8 +93,9 @@ def tile_picked_csketch_none_p_kernel(tc, x_words, x_scales, w1, sg1, sg2, sg3, 
             nc.vector.tensor_copy(gw[:, half * SH : (half + 1) * SH], xw[:].indirect(offs_sb[:, half * SH // 16 : (half + 1) * SH // 16]))
 
         quantize_w1(1)
+        nc.scalar.activation(sg_sb[0][:, :, VH:], sg_sb[0][:, :, VH:], COPY, scale=minus_one)
 
-        y = [sb.tile([P, S], F32, name="y%d" % t, tag="y%d" % t, align_bytes=64) for t in range(PACK)]
+        y = [yp.tile([P, S], F32, name="y%d" % t, offset=t * S * 4, align_bytes=64) for t in range(PACK)]
         pieces = (
             (0, 0, 256, nc.scalar.copy),
             (1, 0, 256, nc.scalar.copy),
@@ -109,7 +118,6 @@ def tile_picked_csketch_none_p_kernel(tc, x_words, x_scales, w1, sg1, sg2, sg3, 
             )
             copy(y[t][:, c0:c1], acc[:])
 
-        nc.scalar.activation(sg_sb[1][:, :, VH:], sg_sb[1][:, :, VH:], COPY, scale=minus_one[:])
 
         tn = [sb.tile([P, PACK, V], F32, name="t%d" % n, align_bytes=64) for n in range(3)]
 
@@ -126,30 +134,29 @@ def tile_picked_csketch_none_p_kernel(tc, x_words, x_scales, w1, sg1, sg2, sg3, 
         diff_ps = ps.tile([P, PACK, P], F32, name="diff_ps", tag="bank0")
         turn(a_ps, tn[0][:, :, VH:], True, True)
         turn(diff_ps, tn[0][:, :, VH:], True, False)
-        a_turned = sb.tile([P, PACK, P], F32, name="a_turned", tag="a_turned", align_bytes=64)
-        nc.scalar.copy(a_turned[:], a_ps[:])
-        hi_ps = ps.tile([P, PACK, VH], F32, name="hi_ps", tag="bank3")
-        turn(hi_ps, a_turned, True, False)
-        look_up(1)
-        b_ps = ps.tile([P, PACK, P], F32, name="b_ps", tag="bank2")
-        turn(diff_ps, tn[1][:, :, VH:], False, True)
-        turn(b_ps, tn[1][:, :, VH:], True, True)
         w2_bf = [sb.tile([P, NH, PACK], BF16, name="w2_bf%d" % a, align_bytes=64) for a in range(2)]
 
         def interleave(dst, planes):
             nc.scalar.copy(dst.rearrange("p (c i) t -> p c t i", i=LINE), planes.rearrange("p t (c i) -> p c t i", i=LINE))
 
-        for a in range(2):
-            interleave(w2_bf[a][:], w2_raw[:, :, a * NH : (a + 1) * NH])
-        turned = sb.tile([P, 2, PACK, P], F32, name="turned", tag="w2_raw", align_bytes=64)
-        gap = turned[:, 0]
-        b_turned = turned[:, 1]
+        interleave(w2_bf[0][:], w2_raw[:, :, :NH])
+        a_turned = w2_raw[:, :, :P]
+        nc.scalar.copy(a_turned, a_ps[:])
+        interleave(w2_bf[1][:], w2_raw[:, :, NH:])
+        nlo_ps = ps.tile([P, PACK, VH], F32, name="nlo_ps", tag="bank3")
+        turn(nlo_ps, a_turned, True, False)
+        look_up(1)
+        b_ps = ps.tile([P, PACK, P], F32, name="b_ps", tag="bank2")
+        turn(diff_ps, tn[1][:, :, VH:], False, True)
+        turn(b_ps, tn[1][:, :, VH:], True, True)
+        gap = w2_raw[:, :, NH : NH + P]
+        b_turned = w2_raw[:, :, NH + P :]
         nc.scalar.activation(gap, diff_ps[:], RELU, scale=-1.0)
         nc.scalar.copy(b_turned, b_ps[:])
-        turn(hi_ps, gap, False, True)
-        nlo_ps = ps.tile([P, PACK, VH], F32, name="nlo_ps", tag="bank1")
-        turn(nlo_ps, gap, True, False)
-        turn(nlo_ps, b_turned, False, True)
+        turn(nlo_ps, gap, False, True)
+        hi_ps = ps.tile([P, PACK, VH], F32, name="hi_ps", tag="bank1")
+        turn(hi_ps, gap, True, False)
+        turn(hi_ps, b_turned, False, True)
         look_up(2)
 
         w2_codes = []
@@ -158,12 +165,13 @@ def tile_picked_csketch_none_p_kernel(tc, x_words, x_scales, w1, sg1, sg2, sg3, 
         def quantize_w2(a):
             cols = slice(a * NH, (a + 1) * NH)
             if a == 0:
-                both = sb.tile([P, 2, NH], U32, name="w2_codes", tag="y0", align_bytes=64)
-                w2_codes.extend([both[:, 0], both[:, 1]])
+                w2_codes.append(sb.tile([P, NH], U32, name="w2_codes0", tag="sg2", align_bytes=64)[:])
+            else:
+                w2_codes.append(yp.tile([P, NH], U32, name="w2_codes1", tag="hi0", offset=0, align_bytes=64)[:])
             nc.vector.quantize_mx(out=w2_codes[a].bitcast(FP8X4), scales=w2_scales[:, cols], in_=w2_bf[a][:].rearrange("p c j -> p (c j)"))
 
-        hi0 = sb.tile([P, PACK, VH], F32, name="hi0", tag="y0", align_bytes=64)
-        lo0 = sb.tile([P, PACK, VH], F32, name="lo0", tag="y1", align_bytes=64)
+        hi0 = yp.tile([P, PACK, VH], F32, name="hi0", tag="hi0", offset=0, align_bytes=64)
+        lo0 = yp.tile([P, PACK, VH], F32, name="lo0", offset=S * 4, align_bytes=64)
         mid0 = sb.tile([P, PACK, VH], F32, name="mid0", tag="mid0", align_bytes=64)
         z0 = sb.tile([P, PACK, VH], F32, name="z0", align_bytes=64)
         woven = sb.tile([P, VH, PACK], F32, name="woven", align_bytes=64)
@@ -173,8 +181,8 @@ def tile_picked_csketch_none_p_kernel(tc, x_words, x_scales, w1, sg1, sg2, sg3, 
         z_codes = [sb.tile([P, VH], U32, name="z_codes%d" % half, align_bytes=64) for half in range(2)]
         z_scales = [sb.tile([P, VH], U8, name="z_scales%d" % half, align_bytes=64) for half in range(2)]
 
-        def clip_above(keys):
-            nc.vector.tensor_tensor(mid1[:, keys], hi_ps[:, :, keys].rearrange("p t v -> p v t"), woven[:, keys], MIN)
+        def clip_below(keys):
+            nc.vector.scalar_tensor_tensor(mid1[:, keys], nlo_ps[:, :, keys].rearrange("p t v -> p v t"), -1.0, woven[:, keys], MULT, MAX)
 
         def quantize_z(half, c0, c1):
             nc.vector.quantize_mx(
@@ -205,17 +213,18 @@ def tile_picked_csketch_none_p_kernel(tc, x_words, x_scales, w1, sg1, sg2, sg3, 
         nc.vector.tensor_tensor(lo0[:], tn[0][:, :, :VH], tn[1][:, :, :VH], MIN)
         nc.vector.tensor_tensor(mid0[:], tn[2][:, :, :VH], hi0[:], MIN)
         quarters = [slice(q * VQ, (q + 1) * VQ) for q in range(2)]
-        clip_above(quarters[0])
-        nc.vector.tensor_tensor(z0[:], lo0[:], mid0[:], MAX)
-        interleave(z_bf[0][:], z0[:])
         quantize_w2(0)
+        for keys in quarters:
+            nc.vector.tensor_tensor(z0[:, :, keys], lo0[:, :, keys], mid0[:, :, keys], MAX)
+            interleave(z_bf[0][:, keys], z0[:, :, keys])
         quantize_w2(1)
+        clip_below(quarters[0])
         quantize_z(0, 0, VH)
         second_product(0, 0, 2, 7, nc.scalar.copy, nc.sync)
         second_product(0, 2, 2, 2, nc.scalar.copy, nc.sync)
-        clip_above(quarters[1])
+        clip_below(quarters[1])
         for keys in quarters:
-            nc.vector.scalar_tensor_tensor(z_bf[1][:, keys], nlo_ps[:, :, keys].rearrange("p t v -> p v t"), -1.0, mid1[:, keys], MULT, MAX)
+            nc.vector.tensor_tensor(z_bf[1][:, keys], hi_ps[:, :, keys].rearrange("p t v -> p v t"), mid1[:, keys], MIN)
         for keys in quarters:
             quantize_z(1, keys.start, keys.stop)
         for u in range(PACK):

@@ -14,6 +14,7 @@ U16 = mybir.dt.uint16
 U8 = mybir.dt.uint8
 FP8X4 = mybir.dt.float8_e4m3fn_x4
 MULT = mybir.AluOpType.mult
+ADD = mybir.AluOpType.add
 MIN = mybir.AluOpType.min
 MAX = mybir.AluOpType.max
 COPY = mybir.ActivationFunctionType.Copy
@@ -58,9 +59,9 @@ def tile_picked_csketch_none_p_kernel(tc, x_words, x_scales, w1, sg1, sg2, sg3, 
         for n, (h, sg) in enumerate(((h1, sg1), (h2, sg2), (h3, sg3))):
             planes = sg.rearrange("(p t) v -> p t v", t=PACK)
             if n == 0:
-                nc.sync.dma_start(sg_sb[n][:, :, VH:], planes[:, :, VH:])
+                nc.sync.dma_start(sg_sb[n][:, :2], planes[:, :2])
                 nc.sync.dma_start(h_sb[n][:], h)
-                nc.sync.dma_start(sg_sb[n][:, :, :VH], planes[:, :, :VH])
+                nc.sync.dma_start(sg_sb[n][:, 2:], planes[:, 2:])
                 continue
             nc.sync.dma_start(h_sb[n][:], h)
             if n == 2:
@@ -93,7 +94,8 @@ def tile_picked_csketch_none_p_kernel(tc, x_words, x_scales, w1, sg1, sg2, sg3, 
             nc.vector.tensor_copy(gw[:, half * SH : (half + 1) * SH], xw[:].indirect(offs_sb[:, half * SH // 16 : (half + 1) * SH // 16]))
 
         quantize_w1(1)
-        nc.scalar.activation(sg_sb[0][:, :, VH:], sg_sb[0][:, :, VH:], COPY, scale=minus_one)
+        nc.scalar.activation(sg_sb[0][:, :2], sg_sb[0][:, :2], COPY, scale=minus_one)
+        nc.gpsimd.tensor_scalar(sg_sb[0][:, 2:], sg_sb[0][:, 2:], -1.0, 0.0, MULT, ADD)
 
         y = [yp.tile([P, S], F32, name="y%d" % t, offset=t * S * 4, align_bytes=64) for t in range(PACK)]
         pieces = (
@@ -121,57 +123,60 @@ def tile_picked_csketch_none_p_kernel(tc, x_words, x_scales, w1, sg1, sg2, sg3, 
 
         tn = [sb.tile([P, PACK, V], F32, name="t%d" % n, align_bytes=64) for n in range(3)]
 
-        def look_up(n):
-            for t in range(PACK):
+        def look_up(n, planes):
+            for t in planes:
                 nc.vector.tensor_tensor(tn[n][:, t, :], y[t][:].indirect(h_sb[n][:]), sg_sb[n][:, t, :], MULT)
 
         def turn(acc, src, start, stop):
             for t in range(PACK):
                 nc.tensor.matmul(acc[:, t, :], src[:, t, :], ident[:], start=start and t == 0, stop=stop and t == PACK - 1, is_transpose=True)
 
-        look_up(0)
-        a_ps = ps.tile([P, PACK, P], F32, name="a_ps", tag="bank7")
-        diff_ps = ps.tile([P, PACK, P], F32, name="diff_ps", tag="bank0")
-        turn(a_ps, tn[0][:, :, VH:], True, True)
-        turn(diff_ps, tn[0][:, :, VH:], True, False)
+        halves = [slice(half * VH, (half + 1) * VH) for half in range(2)]
+        a_ps = [ps.tile([P, PACK, P], F32, name="a_ps%d" % half, tag="bank%d" % (7, 1)[half]) for half in range(2)]
+        diff_ps = [ps.tile([P, PACK, P], F32, name="diff_ps%d" % half, tag="bank%d" % (0, 2)[half]) for half in range(2)]
+        look_up(0, range(PACK))
+        for half, keys in enumerate(halves):
+            turn(a_ps[half], tn[0][:, :, keys], True, True)
+            turn(diff_ps[half], tn[0][:, :, keys], True, False)
         w2_bf = [sb.tile([P, NH, PACK], BF16, name="w2_bf%d" % a, align_bytes=64) for a in range(2)]
 
         def interleave(dst, planes):
             nc.scalar.copy(dst.rearrange("p (c i) t -> p c t i", i=LINE), planes.rearrange("p t (c i) -> p c t i", i=LINE))
 
         interleave(w2_bf[0][:], w2_raw[:, :, :NH])
-        a_turned = w2_raw[:, :, :P]
-        nc.scalar.copy(a_turned, a_ps[:])
+        a_turned = [w2_raw[:, :, half * P : (half + 1) * P] for half in range(2)]
+        for half in range(2):
+            nc.scalar.copy(a_turned[half], a_ps[half][:])
         interleave(w2_bf[1][:], w2_raw[:, :, NH:])
-        nlo_ps = ps.tile([P, PACK, VH], F32, name="nlo_ps", tag="bank3")
-        turn(nlo_ps, a_turned, True, False)
-        look_up(1)
-        b_ps = ps.tile([P, PACK, P], F32, name="b_ps", tag="bank2")
-        turn(diff_ps, tn[1][:, :, VH:], False, True)
+        look_up(1, range(PACK))
+        b_ps = ps.tile([P, PACK, P], F32, name="b_ps", tag="bank5")
+        for half, keys in enumerate(halves):
+            turn(diff_ps[half], tn[1][:, :, keys], False, True)
         turn(b_ps, tn[1][:, :, VH:], True, True)
-        gap = w2_raw[:, :, NH : NH + P]
-        b_turned = w2_raw[:, :, NH + P :]
-        nc.scalar.activation(gap, diff_ps[:], RELU, scale=-1.0)
+        nlo_ps = [ps.tile([P, PACK, VH], F32, name="nlo_ps%d" % half, tag="bank%d" % (3, 4)[half]) for half in range(2)]
+        gap = [w2_raw[:, :, NH + half * P : NH + (half + 1) * P] for half in range(2)]
+        for half in range(2):
+            turn(nlo_ps[half], a_turned[half], True, False)
+            nc.scalar.activation(gap[half], diff_ps[half][:], RELU, scale=-1.0)
+            turn(nlo_ps[half], gap[half], False, True)
+        b_turned = a_turned[0]
         nc.scalar.copy(b_turned, b_ps[:])
-        turn(nlo_ps, gap, False, True)
-        hi_ps = ps.tile([P, PACK, VH], F32, name="hi_ps", tag="bank1")
-        turn(hi_ps, gap, True, False)
+        hi_ps = ps.tile([P, PACK, VH], F32, name="hi_ps", tag="bank6")
+        turn(hi_ps, gap[1], True, False)
         turn(hi_ps, b_turned, False, True)
-        look_up(2)
+        hi0 = yp.tile([P, PACK, VH], F32, name="hi0", offset=0, align_bytes=64)
+        look_up(2, range(1))
+        nc.vector.scalar_tensor_tensor(hi0[:], tn[0][:, :, :VH], -1.0, tn[1][:, :, :VH], MULT, MAX)
+        look_up(2, range(1, PACK))
 
         w2_codes = []
         w2_scales = sb.tile([P, N], U8, name="w2_scales", align_bytes=64)
 
         def quantize_w2(a):
             cols = slice(a * NH, (a + 1) * NH)
-            if a == 0:
-                w2_codes.append(sb.tile([P, NH], U32, name="w2_codes0", tag="sg2", align_bytes=64)[:])
-            else:
-                w2_codes.append(yp.tile([P, NH], U32, name="w2_codes1", tag="hi0", offset=0, align_bytes=64)[:])
+            w2_codes.append(yp.tile([P, NH], U32, name="w2_codes%d" % a, offset=(2 + a) * S * 4, align_bytes=64)[:])
             nc.vector.quantize_mx(out=w2_codes[a].bitcast(FP8X4), scales=w2_scales[:, cols], in_=w2_bf[a][:].rearrange("p c j -> p (c j)"))
 
-        hi0 = yp.tile([P, PACK, VH], F32, name="hi0", tag="hi0", offset=0, align_bytes=64)
-        lo0 = yp.tile([P, PACK, VH], F32, name="lo0", offset=S * 4, align_bytes=64)
         mid0 = sb.tile([P, PACK, VH], F32, name="mid0", tag="mid0", align_bytes=64)
         z0 = sb.tile([P, PACK, VH], F32, name="z0", align_bytes=64)
         woven = sb.tile([P, VH, PACK], F32, name="woven", align_bytes=64)
@@ -182,7 +187,7 @@ def tile_picked_csketch_none_p_kernel(tc, x_words, x_scales, w1, sg1, sg2, sg3, 
         z_scales = [sb.tile([P, VH], U8, name="z_scales%d" % half, align_bytes=64) for half in range(2)]
 
         def clip_below(keys):
-            nc.vector.scalar_tensor_tensor(mid1[:, keys], nlo_ps[:, :, keys].rearrange("p t v -> p v t"), -1.0, woven[:, keys], MULT, MAX)
+            nc.vector.scalar_tensor_tensor(mid1[:, keys], nlo_ps[1][:, :, keys].rearrange("p t v -> p v t"), -1.0, woven[:, keys], MULT, MAX)
 
         def quantize_z(half, c0, c1):
             nc.vector.quantize_mx(
@@ -209,26 +214,24 @@ def tile_picked_csketch_none_p_kernel(tc, x_words, x_scales, w1, sg1, sg2, sg3, 
             copy_engine(res[:], acc[:])
             store_engine.dma_start(out_rows[:, u0 : u0 + count, half * VH : (half + 1) * VH], res[:])
 
-        nc.vector.tensor_tensor(hi0[:], tn[0][:, :, :VH], tn[1][:, :, :VH], MAX)
-        nc.vector.tensor_tensor(lo0[:], tn[0][:, :, :VH], tn[1][:, :, :VH], MIN)
-        nc.vector.tensor_tensor(mid0[:], tn[2][:, :, :VH], hi0[:], MIN)
-        quarters = [slice(q * VQ, (q + 1) * VQ) for q in range(2)]
         quantize_w2(0)
-        for keys in quarters:
-            nc.vector.tensor_tensor(z0[:, :, keys], lo0[:, :, keys], mid0[:, :, keys], MAX)
-            interleave(z_bf[0][:, keys], z0[:, :, keys])
+        nc.vector.tensor_tensor(mid0[:], tn[2][:, :, :VH], hi0[:], MIN)
         quantize_w2(1)
+        quarters = [slice(q * VQ, (q + 1) * VQ) for q in range(2)]
+        for keys in quarters:
+            nc.vector.scalar_tensor_tensor(z0[:, :, keys], nlo_ps[0][:, :, keys], -1.0, mid0[:, :, keys], MULT, MAX)
+            interleave(z_bf[0][:, keys], z0[:, :, keys])
         clip_below(quarters[0])
+        clip_below(quarters[1])
         quantize_z(0, 0, VH)
         second_product(0, 0, 2, 7, nc.scalar.copy, nc.sync)
-        second_product(0, 2, 2, 2, nc.scalar.copy, nc.sync)
-        clip_below(quarters[1])
+        second_product(0, 2, 2, 0, nc.scalar.copy, nc.sync)
         for keys in quarters:
             nc.vector.tensor_tensor(z_bf[1][:, keys], hi_ps[:, :, keys].rearrange("p t v -> p v t"), mid1[:, keys], MIN)
         for keys in quarters:
             quantize_z(1, keys.start, keys.stop)
         for u in range(PACK):
             if u % 2 == 0:
-                second_product(1, u, 1, (4, 5, 6, 0)[u], nc.scalar.copy, nc.scalar)
+                second_product(1, u, 1, (1, 2, 5, 3)[u], nc.scalar.copy, nc.scalar)
             else:
-                second_product(1, u, 1, (4, 5, 6, 0)[u], nc.vector.tensor_copy, nc.sync)
+                second_product(1, u, 1, (1, 2, 5, 3)[u], nc.vector.tensor_copy, nc.sync)

@@ -221,6 +221,17 @@ def tile_picked_csketch_none_p_kernel(tc, x_words, x_scales, w1, sg1, sg2, sg3, 
         for keys in quarters:
             nc.vector.scalar_tensor_tensor(z0[:, :, keys], nlo_ps[0][:, :, keys], -1.0, mid0[:, :, keys], MULT, MAX)
             interleave(z_bf[0][:, keys], z0[:, :, keys])
+        for cols in (S, SH):
+            warm = ps.tile([P, cols], F32, name="warm%d" % cols, tag="bank3")
+            nc.tensor.matmul_mx(
+                out=warm[:],
+                lhsT=w1_codes[:, :P].bitcast(FP8X4),
+                lhsT_scale=w1_scales[:, :P],
+                rhs=gw[:, :cols].bitcast(FP8X4),
+                rhs_scale=gs[:, :cols],
+                start=True,
+                stop=True,
+            )
         clip_below(quarters[0])
         clip_below(quarters[1])
         quantize_z(0, 0, VH)

@@ -90,8 +90,8 @@ def tile_picked_csketch_none_p_kernel(tc, x_words, x_scales, w1, sg1, sg2, sg3, 
         quantize_w1(0)
 
         gw = sb.tile([P, S], U32, name="gw", align_bytes=64)
-        for half in range(2):
-            nc.vector.tensor_copy(gw[:, half * SH : (half + 1) * SH], xw[:].indirect(offs_sb[:, half * SH // 16 : (half + 1) * SH // 16]))
+        for c0, c1 in ((0, 256), (256, 384), (384, 512)):
+            nc.vector.tensor_copy(gw[:, c0:c1], xw[:].indirect(offs_sb[:, c0 // 16 : c1 // 16]))
 
         quantize_w1(1)
         nc.scalar.activation(sg_sb[0][:, :2], sg_sb[0][:, :2], COPY, scale=minus_one)
@@ -100,15 +100,17 @@ def tile_picked_csketch_none_p_kernel(tc, x_words, x_scales, w1, sg1, sg2, sg3, 
         y = [yp.tile([P, S], F32, name="y%d" % t, offset=t * S * 4, align_bytes=64) for t in range(PACK)]
         pieces = (
             (0, 0, 256, nc.scalar.copy),
-            (1, 0, 256, nc.scalar.copy),
-            (0, 256, 384, nc.vector.tensor_copy),
+            (0, 256, 384, nc.scalar.copy),
+            (1, 0, 256, nc.vector.tensor_copy),
             (0, 384, 512, nc.scalar.copy),
             (1, 256, 512, nc.scalar.copy),
-            (2, 0, 512, nc.scalar.copy),
-            (3, 0, 512, nc.scalar.copy),
+            (2, 0, 256, nc.scalar.copy),
+            (2, 256, 512, nc.scalar.copy),
+            (3, 0, 256, nc.scalar.copy),
+            (3, 256, 512, nc.scalar.copy),
         )
         for n, (t, c0, c1, copy) in enumerate(pieces):
-            acc = ps.tile([P, c1 - c0], F32, name="y_ps%d" % n, tag="bank%d" % n)
+            acc = ps.tile([P, c1 - c0], F32, name="y_ps%d" % n, tag="bank%d" % (n % 8))
             nc.tensor.matmul_mx(
                 out=acc[:],
                 lhsT=w1_codes[:, t * P : (t + 1) * P].bitcast(FP8X4),
@@ -132,8 +134,8 @@ def tile_picked_csketch_none_p_kernel(tc, x_words, x_scales, w1, sg1, sg2, sg3, 
                 nc.tensor.matmul(acc[:, t, :], src[:, t, :], ident[:], start=start and t == 0, stop=stop and t == PACK - 1, is_transpose=True)
 
         halves = [slice(half * VH, (half + 1) * VH) for half in range(2)]
-        a_ps = [ps.tile([P, PACK, P], F32, name="a_ps%d" % half, tag="bank%d" % (7, 1)[half]) for half in range(2)]
-        diff_ps = [ps.tile([P, PACK, P], F32, name="diff_ps%d" % half, tag="bank%d" % (0, 2)[half]) for half in range(2)]
+        a_ps = [ps.tile([P, PACK, P], F32, name="a_ps%d" % half, tag="bank%d" % (3, 1)[half]) for half in range(2)]
+        diff_ps = [ps.tile([P, PACK, P], F32, name="diff_ps%d" % half, tag="bank%d" % (4, 2)[half]) for half in range(2)]
         look_up(0, range(PACK))
         for half, keys in enumerate(halves):
             turn(a_ps[half], tn[0][:, :, keys], True, True)
@@ -153,7 +155,7 @@ def tile_picked_csketch_none_p_kernel(tc, x_words, x_scales, w1, sg1, sg2, sg3, 
         for half, keys in enumerate(halves):
             turn(diff_ps[half], tn[1][:, :, keys], False, True)
         turn(b_ps, tn[1][:, :, VH:], True, True)
-        nlo_ps = [ps.tile([P, PACK, VH], F32, name="nlo_ps%d" % half, tag="bank%d" % (3, 4)[half]) for half in range(2)]
+        nlo_ps = [ps.tile([P, PACK, VH], F32, name="nlo_ps%d" % half, tag="bank%d" % (7, 0)[half]) for half in range(2)]
         gap = [w2_raw[:, :, NH + half * P : NH + (half + 1) * P] for half in range(2)]
         for half in range(2):
             turn(nlo_ps[half], a_turned[half], True, False)
@@ -222,7 +224,7 @@ def tile_picked_csketch_none_p_kernel(tc, x_words, x_scales, w1, sg1, sg2, sg3, 
             nc.vector.scalar_tensor_tensor(z0[:, :, keys], nlo_ps[0][:, :, keys], -1.0, mid0[:, :, keys], MULT, MAX)
             interleave(z_bf[0][:, keys], z0[:, :, keys])
         for cols in (S, SH):
-            warm = ps.tile([P, cols], F32, name="warm%d" % cols, tag="bank3")
+            warm = ps.tile([P, cols], F32, name="warm%d" % cols, tag="bank7")
             nc.tensor.matmul_mx(
                 out=warm[:],
                 lhsT=w1_codes[:, :P].bitcast(FP8X4),
@@ -235,14 +237,14 @@ def tile_picked_csketch_none_p_kernel(tc, x_words, x_scales, w1, sg1, sg2, sg3, 
         clip_below(quarters[0])
         clip_below(quarters[1])
         quantize_z(0, 0, VH)
-        second_product(0, 0, 2, 7, nc.scalar.copy, nc.sync)
-        second_product(0, 2, 2, 0, nc.scalar.copy, nc.sync)
+        second_product(0, 0, 2, 3, nc.scalar.copy, nc.sync)
+        second_product(0, 2, 2, 4, nc.scalar.copy, nc.sync)
         for keys in quarters:
             nc.vector.tensor_tensor(z_bf[1][:, keys], hi_ps[:, :, keys].rearrange("p t v -> p v t"), mid1[:, keys], MIN)
         for keys in quarters:
             quantize_z(1, keys.start, keys.stop)
         for u in range(PACK):
             if u % 2 == 0:
-                second_product(1, u, 1, (1, 2, 5, 3)[u], nc.scalar.copy, nc.scalar)
+                second_product(1, u, 1, (1, 2, 5, 7)[u], nc.scalar.copy, nc.scalar)
             else:
-                second_product(1, u, 1, (1, 2, 5, 3)[u], nc.vector.tensor_copy, nc.sync)
+                second_product(1, u, 1, (1, 2, 5, 7)[u], nc.vector.tensor_copy, nc.sync)

@@ -14,7 +14,6 @@ U16 = mybir.dt.uint16
 U8 = mybir.dt.uint8
 FP8X4 = mybir.dt.float8_e4m3fn_x4
 MULT = mybir.AluOpType.mult
-ADD = mybir.AluOpType.add
 MIN = mybir.AluOpType.min
 MAX = mybir.AluOpType.max
 COPY = mybir.ActivationFunctionType.Copy
@@ -26,7 +25,6 @@ LINE = 4
 W1_VECTOR_ROWS = 48
 VH = V // 2
 VQ = V // 4
-SH = S // 2
 NH = N // 2
 
 
@@ -34,7 +32,6 @@ def tile_picked_csketch_none_p_kernel(tc, x_words, x_scales, w1, sg1, sg2, sg3, 
     nc = tc.nc
     with ExitStack() as ctx:
         sb = ctx.enter_context(tc.tile_pool(name="sb", bufs=1))
-        yp = ctx.enter_context(tc.tile_pool(name="yp", bufs=1))
         ps = ctx.enter_context(tc.psum_pool(name="ps", bufs=1))
 
         offs_sb = sb.tile([P, S // 16], U16, name="offs_sb")
@@ -42,31 +39,30 @@ def tile_picked_csketch_none_p_kernel(tc, x_words, x_scales, w1, sg1, sg2, sg3, 
         xw = sb.tile([P, T], U32, name="xw", align_bytes=64)
         xs = sb.tile([P, T], U8, name="xs", align_bytes=64)
         w1_raw = sb.tile([P, PACK, H], F32, name="w1_raw", align_bytes=64)
-        w2_raw = sb.tile([P, PACK, N], F32, name="w2_raw", tag="w2_raw", align_bytes=64)
-        sg_sb = [sb.tile([P, PACK, V], F32, name="sg%d_sb" % n, tag="sg%d" % n, align_bytes=64) for n in range(3)]
-
+        w2_raw = [sb.tile([P, PACK, NH], F32, name="w2_raw%d" % a, align_bytes=64) for a in range(2)]
+        w2_rows = w2.rearrange("(p j) c -> p j c", j=PACK)
+        room = ctx.enter_context(tc.tile_pool(name="room", bufs=1))
+        sg1_sb = [room.tile([P, 2, V], F32, name="sg1_%d" % pair, offset=pair * 2 * V * 4, align_bytes=64) for pair in range(2)]
+        sg2_sb = sb.tile([P, PACK, V], F32, name="sg2_sb", align_bytes=64)
+        sg3_sb = sb.tile([P, PACK, V], F32, name="sg3_sb", align_bytes=64)
         ident = sb.tile([P, P], F32, name="ident", align_bytes=64)
         make_identity(nc, ident[:])
-        y_room = yp.tile([P, PACK * S], F32, name="y_room", offset=0, align_bytes=64)
-        minus_one = y_room[:, 0:1]
-        nc.gpsimd.memset(minus_one, -1.0)
+        sg_planes = [sg.rearrange("(p t) v -> p t v", t=PACK) for sg in (sg1, sg2, sg3)]
         nc.vector.memset(xs[:].bitcast(I32), 0)
         nc.sync.dma_start(w1_raw[:], w1.rearrange("(p j) c -> p j c", j=PACK))
         nc.sync.dma_start(offs_sb[:], offs)
         for q in range(4):
             nc.sync.dma_start(xs[q:P:32, :].bitcast(I32), x_scales[0, q:16:4, :].bitcast(I32))
         nc.sync.dma_start(xw[:].bitcast(I32), x_words[0].rearrange("p n t -> p (n t)").bitcast(I32))
-        for n, (h, sg) in enumerate(((h1, sg1), (h2, sg2), (h3, sg3))):
-            planes = sg.rearrange("(p t) v -> p t v", t=PACK)
-            if n == 0:
-                nc.sync.dma_start(sg_sb[n][:, :2], planes[:, :2])
-                nc.sync.dma_start(h_sb[n][:], h)
-                nc.sync.dma_start(sg_sb[n][:, 2:], planes[:, 2:])
-                continue
-            nc.sync.dma_start(h_sb[n][:], h)
-            if n == 2:
-                nc.sync.dma_start(w2_raw[:], w2.rearrange("(p j) c -> p j c", j=PACK))
-            nc.sync.dma_start(sg_sb[n][:], planes)
+        nc.sync.dma_start(w2_raw[0][:], w2_rows[:, :, :NH])
+        nc.sync.dma_start(sg1_sb[0][:], sg_planes[0][:, :2])
+        nc.sync.dma_start(h_sb[0][:], h1)
+        nc.sync.dma_start(sg1_sb[1][:], sg_planes[0][:, 2:])
+        nc.sync.dma_start(h_sb[1][:], h2)
+        nc.sync.dma_start(h_sb[2][:], h3)
+        nc.sync.dma_start(sg3_sb[:], sg_planes[2])
+        nc.sync.dma_start(sg2_sb[:], sg_planes[1])
+        nc.sync.dma_start(w2_raw[1][:], w2_rows[:, :, NH:])
 
         gs = sb.tile([P, S], U8, name="gs", align_bytes=64)
         nc.vector.tensor_copy(gs[:], xs[:].indirect(offs_sb[:]))
@@ -94,15 +90,13 @@ def tile_picked_csketch_none_p_kernel(tc, x_words, x_scales, w1, sg1, sg2, sg3, 
             nc.vector.tensor_copy(gw[:, c0:c1], xw[:].indirect(offs_sb[:, c0 // 16 : c1 // 16]))
 
         quantize_w1(1)
-        nc.scalar.activation(sg_sb[0][:, :2], sg_sb[0][:, :2], COPY, scale=minus_one)
-        nc.gpsimd.tensor_scalar(sg_sb[0][:, 2:], sg_sb[0][:, 2:], -1.0, 0.0, MULT, ADD)
 
-        y = [yp.tile([P, S], F32, name="y%d" % t, offset=t * S * 4, align_bytes=64) for t in range(PACK)]
+        y = [sb.tile([P, S], F32, name="y%d" % t, align_bytes=64) for t in range(PACK)]
         pieces = (
             (0, 0, 256, nc.scalar.copy),
             (0, 256, 384, nc.scalar.copy),
-            (1, 0, 256, nc.vector.tensor_copy),
             (0, 384, 512, nc.scalar.copy),
+            (1, 0, 256, nc.scalar.copy),
             (1, 256, 512, nc.scalar.copy),
             (2, 0, 256, nc.scalar.copy),
             (2, 256, 512, nc.scalar.copy),
@@ -122,74 +116,24 @@ def tile_picked_csketch_none_p_kernel(tc, x_words, x_scales, w1, sg1, sg2, sg3, 
             )
             copy(y[t][:, c0:c1], acc[:])
 
-
-        tn = [sb.tile([P, PACK, V], F32, name="t%d" % n, align_bytes=64) for n in range(3)]
-
-        def look_up(n, planes):
-            for t in planes:
-                nc.vector.tensor_tensor(tn[n][:, t, :], y[t][:].indirect(h_sb[n][:]), sg_sb[n][:, t, :], MULT)
-
-        def turn(acc, src, start, stop):
-            for t in range(PACK):
-                nc.tensor.matmul(acc[:, t, :], src[:, t, :], ident[:], start=start and t == 0, stop=stop and t == PACK - 1, is_transpose=True)
-
-        halves = [slice(half * VH, (half + 1) * VH) for half in range(2)]
-        a_ps = [ps.tile([P, PACK, P], F32, name="a_ps%d" % half, tag="bank%d" % (3, 1)[half]) for half in range(2)]
-        diff_ps = [ps.tile([P, PACK, P], F32, name="diff_ps%d" % half, tag="bank%d" % (4, 2)[half]) for half in range(2)]
-        look_up(0, range(PACK))
-        for half, keys in enumerate(halves):
-            turn(a_ps[half], tn[0][:, :, keys], True, True)
-            turn(diff_ps[half], tn[0][:, :, keys], True, False)
-        w2_bf = [sb.tile([P, NH, PACK], BF16, name="w2_bf%d" % a, align_bytes=64) for a in range(2)]
-
-        def interleave(dst, planes):
-            nc.scalar.copy(dst.rearrange("p (c i) t -> p c t i", i=LINE), planes.rearrange("p t (c i) -> p c t i", i=LINE))
-
-        interleave(w2_bf[0][:], w2_raw[:, :, :NH])
-        a_turned = [w2_raw[:, :, half * P : (half + 1) * P] for half in range(2)]
-        for half in range(2):
-            nc.scalar.copy(a_turned[half], a_ps[half][:])
-        interleave(w2_bf[1][:], w2_raw[:, :, NH:])
-        look_up(1, range(PACK))
-        b_ps = ps.tile([P, PACK, P], F32, name="b_ps", tag="bank5")
-        for half, keys in enumerate(halves):
-            turn(diff_ps[half], tn[1][:, :, keys], False, True)
-        turn(b_ps, tn[1][:, :, VH:], True, True)
-        nlo_ps = [ps.tile([P, PACK, VH], F32, name="nlo_ps%d" % half, tag="bank%d" % (7, 0)[half]) for half in range(2)]
-        gap = [w2_raw[:, :, NH + half * P : NH + (half + 1) * P] for half in range(2)]
-        for half in range(2):
-            turn(nlo_ps[half], a_turned[half], True, False)
-            nc.scalar.activation(gap[half], diff_ps[half][:], RELU, scale=-1.0)
-            turn(nlo_ps[half], gap[half], False, True)
-        b_turned = a_turned[0]
-        nc.scalar.copy(b_turned, b_ps[:])
-        hi_ps = ps.tile([P, PACK, VH], F32, name="hi_ps", tag="bank6")
-        turn(hi_ps, gap[1], True, False)
-        turn(hi_ps, b_turned, False, True)
-        hi0 = yp.tile([P, PACK, VH], F32, name="hi0", offset=0, align_bytes=64)
-        look_up(2, range(1))
-        nc.vector.scalar_tensor_tensor(hi0[:], tn[0][:, :, :VH], -1.0, tn[1][:, :, :VH], MULT, MAX)
-        look_up(2, range(1, PACK))
-
-        w2_codes = []
-        w2_scales = sb.tile([P, N], U8, name="w2_scales", align_bytes=64)
-
-        def quantize_w2(a):
-            cols = slice(a * NH, (a + 1) * NH)
-            w2_codes.append(yp.tile([P, NH], U32, name="w2_codes%d" % a, offset=(2 + a) * S * 4, align_bytes=64)[:])
-            nc.vector.quantize_mx(out=w2_codes[a].bitcast(FP8X4), scales=w2_scales[:, cols], in_=w2_bf[a][:].rearrange("p c j -> p (c j)"))
-
-        mid0 = sb.tile([P, PACK, VH], F32, name="mid0", tag="mid0", align_bytes=64)
-        z0 = sb.tile([P, PACK, VH], F32, name="z0", align_bytes=64)
-        woven = sb.tile([P, VH, PACK], F32, name="woven", align_bytes=64)
-        mid1 = sb.tile([P, VH, PACK], F32, name="mid1", align_bytes=64)
-        interleave(woven[:], tn[2][:, :, VH:])
-        z_bf = [sb.tile([P, VH, PACK], BF16, name="z_bf%d" % half, tag="z_bf%d" % half, align_bytes=64) for half in range(2)]
+        quarters = [slice(q * VQ, (q + 1) * VQ) for q in range(2)]
+        t1 = room.tile([P, PACK, V], F32, name="t1", offset=6144, align_bytes=64)
+        g2 = sb.tile([P, PACK, V], F32, name="g2", align_bytes=64)
+        n2 = [sb.tile([P, 2, V], F32, name="n2_0", align_bytes=64), room.tile([P, 2, V], F32, name="n2_1", offset=4096, align_bytes=64)]
+        t3 = [sb.tile([P, PACK, VH], F32, name="t3_0", align_bytes=64), room.tile([P, PACK, VH], F32, name="t3_1", offset=6144, align_bytes=64)]
+        g3 = sb.tile([P, PACK, VH], F32, name="g3", align_bytes=64)
+        z_bf = [sb.tile([P, VH, PACK], BF16, name="z_bf%d" % half, align_bytes=64) for half in range(2)]
         z_codes = [sb.tile([P, VH], U32, name="z_codes%d" % half, align_bytes=64) for half in range(2)]
         z_scales = [sb.tile([P, VH], U8, name="z_scales%d" % half, align_bytes=64) for half in range(2)]
+        w2_bf = [sb.tile([P, NH, PACK], BF16, name="w2_bf0", align_bytes=64), room.tile([P, NH, PACK], BF16, name="w2_bf1", offset=4096, align_bytes=64)]
+        w2_codes = [sb.tile([P, NH], U32, name="w2_codes%d" % a, align_bytes=64) for a in range(2)]
+        w2_scales = sb.tile([P, N], U8, name="w2_scales", align_bytes=64)
 
-        def clip_below(keys):
-            nc.vector.scalar_tensor_tensor(mid1[:, keys], nlo_ps[1][:, :, keys].rearrange("p t v -> p v t"), -1.0, woven[:, keys], MULT, MAX)
+        def interleave(copy, dst, planes):
+            copy(dst.rearrange("p (c i) t -> p c t i", i=LINE), planes.rearrange("p t (c i) -> p c t i", i=LINE))
+
+        def quantize_w2(a):
+            nc.vector.quantize_mx(out=w2_codes[a][:].bitcast(FP8X4), scales=w2_scales[:, a * NH : (a + 1) * NH], in_=w2_bf[a][:].rearrange("p c j -> p (c j)"))
 
         def quantize_z(half, c0, c1):
             nc.vector.quantize_mx(
@@ -216,35 +160,77 @@ def tile_picked_csketch_none_p_kernel(tc, x_words, x_scales, w1, sg1, sg2, sg3, 
             copy_engine(res[:], acc[:])
             store_engine.dma_start(out_rows[:, u0 : u0 + count, half * VH : (half + 1) * VH], res[:])
 
+        def look_up(dst, t, offsets, signs):
+            nc.vector.tensor_tensor(dst[:, t, :], y[t][:].indirect(offsets), signs, MULT)
+
+        def turn(acc, t, src, start, stop):
+            nc.tensor.matmul(acc[:, t, :], src, ident[:], start=start, stop=stop, is_transpose=True)
+
+        t1_ps = ps.tile([P, PACK, P], F32, name="t1_ps", tag="bank1")
+        diff_ps = ps.tile([P, PACK, P], F32, name="diff_ps", tag="bank3")
+        n2_ps = ps.tile([P, PACK, P], F32, name="n2_ps", tag="bank4")
+        hi_ps = ps.tile([P, PACK, VH], F32, name="hi_ps", tag="bank2")
+        nlo_ps = ps.tile([P, PACK, VH], F32, name="nlo_ps", tag="bank5")
+        t1_turned = sb.tile([P, PACK, P], F32, name="t1_turned", align_bytes=64)
+        n2_turned = sb.tile([P, PACK, P], F32, name="n2_turned", align_bytes=64)
+        gap = sb.tile([P, PACK, P], F32, name="gap", align_bytes=64)
+        lo0 = sb.tile([P, PACK, VH], F32, name="lo0", align_bytes=64)
+        hi0 = sb.tile([P, PACK, VH], F32, name="hi0", align_bytes=64)
+        mid0 = sb.tile([P, PACK, VH], F32, name="mid0", align_bytes=64)
+        z0 = sb.tile([P, PACK, VH], F32, name="z0", align_bytes=64)
+        mid1 = sb.tile([P, PACK, VH], F32, name="mid1", align_bytes=64)
+
+        interleave(nc.vector.tensor_copy, w2_bf[0][:], w2_raw[0][:])
         quantize_w2(0)
-        nc.vector.tensor_tensor(mid0[:], tn[2][:, :, :VH], hi0[:], MIN)
+        for t in range(PACK):
+            look_up(t1, t, h_sb[0][:], sg1_sb[t // 2][:, t % 2, :])
+            turn(diff_ps, t, t1[:, t, VH:], t == 0, False)
+            turn(t1_ps, t, t1[:, t, VH:], t == 0, t == PACK - 1)
+        for t in range(PACK):
+            nc.scalar.activation(g2[:, t, :], y[t][:].indirect(h_sb[1][:]), COPY)
+        nc.scalar.copy(t1_turned[:], t1_ps[:])
+        for t in range(PACK):
+            nc.scalar.activation(g3[:, t, :], y[t][:].indirect(h_sb[2][:, VH // 16 :]), COPY)
+        for pair in range(2):
+            planes = slice(2 * pair, 2 * pair + 2)
+            for t in range(2 * pair, 2 * pair + 2):
+                look_up(t3[0], t, h_sb[2][:, : VH // 16], sg3_sb[:, t, :VH])
+            nc.vector.scalar_tensor_tensor(n2[pair][:], g2[:, planes], -1.0, sg2_sb[:, planes], MULT, MULT)
+            for t in range(2 * pair, 2 * pair + 2):
+                turn(diff_ps, t, n2[pair][:, t % 2, VH:], False, t == PACK - 1)
+            for t in range(2 * pair, 2 * pair + 2):
+                turn(n2_ps, t, n2[pair][:, t % 2, VH:], t == 0, t == PACK - 1)
+        for t in range(PACK):
+            turn(hi_ps, t, t1_turned[:, t, :], t == 0, False)
+        nc.scalar.activation(gap[:], diff_ps[:], RELU, scale=-1.0)
+        nc.scalar.copy(n2_turned[:], n2_ps[:])
+        interleave(nc.scalar.copy, w2_bf[1][:], w2_raw[1][:])
+        for t in range(PACK):
+            turn(hi_ps, t, gap[:, t, :], False, t == PACK - 1)
+        for t in range(PACK):
+            turn(nlo_ps, t, gap[:, t, :], t == 0, False)
+        for t in range(PACK):
+            turn(nlo_ps, t, n2_turned[:, t, :], False, t == PACK - 1)
+
+        for pair in range(2):
+            planes = slice(2 * pair, 2 * pair + 2)
+            nc.vector.scalar_tensor_tensor(lo0[:, planes], n2[pair][:, :, :VH], -1.0, t1[:, planes, :VH], MULT, MIN)
+            nc.vector.scalar_tensor_tensor(hi0[:, planes], n2[pair][:, :, :VH], -1.0, t1[:, planes, :VH], MULT, MAX)
+        nc.vector.tensor_tensor(mid0[:], t3[0][:], lo0[:], MAX)
+        nc.vector.tensor_tensor(t3[1][:], g3[:], sg3_sb[:, :, VH:], MULT)
+        nc.vector.tensor_tensor(z0[:], mid0[:], hi0[:], MIN)
+        interleave(nc.scalar.copy, z_bf[0][:], z0[:])
+        nc.vector.tensor_tensor(mid1[:], hi_ps[:], t3[1][:], MIN)
         quantize_w2(1)
-        quarters = [slice(q * VQ, (q + 1) * VQ) for q in range(2)]
-        for keys in quarters:
-            nc.vector.scalar_tensor_tensor(z0[:, :, keys], nlo_ps[0][:, :, keys], -1.0, mid0[:, :, keys], MULT, MAX)
-            interleave(z_bf[0][:, keys], z0[:, :, keys])
-        for cols in (S, SH):
-            warm = ps.tile([P, cols], F32, name="warm%d" % cols, tag="bank7")
-            nc.tensor.matmul_mx(
-                out=warm[:],
-                lhsT=w1_codes[:, :P].bitcast(FP8X4),
-                lhsT_scale=w1_scales[:, :P],
-                rhs=gw[:, :cols].bitcast(FP8X4),
-                rhs_scale=gs[:, :cols],
-                start=True,
-                stop=True,
-            )
-        clip_below(quarters[0])
-        clip_below(quarters[1])
         quantize_z(0, 0, VH)
-        second_product(0, 0, 2, 3, nc.scalar.copy, nc.sync)
-        second_product(0, 2, 2, 4, nc.scalar.copy, nc.sync)
+        second_product(0, 0, 2, 6, nc.scalar.copy, nc.sync)
+        second_product(0, 2, 2, 7, nc.scalar.copy, nc.sync)
         for keys in quarters:
-            nc.vector.tensor_tensor(z_bf[1][:, keys], hi_ps[:, :, keys].rearrange("p t v -> p v t"), mid1[:, keys], MIN)
+            nc.vector.scalar_tensor_tensor(z_bf[1][:, keys], nlo_ps[:, :, keys].rearrange("p t v -> p v t"), -1.0, mid1[:, :, keys].rearrange("p t v -> p v t"), MULT, MAX)
         for keys in quarters:
             quantize_z(1, keys.start, keys.stop)
         for u in range(PACK):
             if u % 2 == 0:
-                second_product(1, u, 1, (1, 2, 5, 7)[u], nc.scalar.copy, nc.scalar)
+                second_product(1, u, 1, (1, 3, 4, 0)[u], nc.scalar.copy, nc.scalar)
             else:
-                second_product(1, u, 1, (1, 2, 5, 7)[u], nc.vector.tensor_copy, nc.sync)
+                second_product(1, u, 1, (1, 3, 4, 0)[u], nc.vector.tensor_copy, nc.sync)

@@ -85,28 +85,21 @@ def tile_picked_csketch_none_p_kernel(tc, x_words, x_scales, w1, sg1, sg2, sg3, 
 
         quantize_w1(0)
 
-        gw = sb.tile([P, S], U32, name="gw", align_bytes=64)
-        for c0, c1 in ((0, 256), (256, 384), (384, 512)):
-            nc.vector.tensor_copy(gw[:, c0:c1], xw[:].indirect(offs_sb[:, c0 // 16 : c1 // 16]))
-
         quantize_w1(1)
 
+        gw = sb.tile([P, S], U32, name="gw", align_bytes=64)
+        for c0 in range(0, S, P):
+            nc.vector.tensor_copy(gw[:, c0 : c0 + P], xw[:].indirect(offs_sb[:, c0 // 16 : (c0 + P) // 16]))
+
         y = [sb.tile([P, S], F32, name="y%d" % t, align_bytes=64) for t in range(PACK)]
-        pieces = (
-            (0, 0, 256, nc.scalar.copy),
-            (0, 256, 384, nc.scalar.copy),
-            (0, 384, 512, nc.scalar.copy),
-            (1, 0, 256, nc.scalar.copy),
-            (1, 256, 512, nc.scalar.copy),
-            (2, 0, 256, nc.scalar.copy),
-            (2, 256, 512, nc.scalar.copy),
-            (3, 0, 256, nc.scalar.copy),
-            (3, 256, 512, nc.scalar.copy),
-        )
-        for n, (t, c0, c1, copy) in enumerate(pieces):
-            acc = ps.tile([P, c1 - c0], F32, name="y_ps%d" % n, tag="bank%d" % (n % 8))
+        banks = {}
+
+        def first_product(t, c0, c1, bank, b0, b1):
+            if c0 == b0:
+                banks[bank] = ps.tile([P, b1 - b0], F32, name="y_ps%d_%d" % (t, b0), tag="bank%d" % bank)
+            acc = banks[bank]
             nc.tensor.matmul_mx(
-                out=acc[:],
+                out=acc[:, c0 - b0 : c1 - b0],
                 lhsT=w1_codes[:, t * P : (t + 1) * P].bitcast(FP8X4),
                 lhsT_scale=w1_scales[:, t * P : (t + 1) * P],
                 rhs=gw[:, c0:c1].bitcast(FP8X4),
@@ -114,7 +107,21 @@ def tile_picked_csketch_none_p_kernel(tc, x_words, x_scales, w1, sg1, sg2, sg3, 
                 start=True,
                 stop=True,
             )
-            copy(y[t][:, c0:c1], acc[:])
+            if c1 == b1:
+                nc.scalar.copy(y[t][:, b0:b1], acc[:])
+
+        first_product(0, 0, 128, 0, 0, 256)
+        first_product(1, 0, 128, 1, 0, 256)
+        first_product(0, 128, 256, 0, 0, 256)
+        first_product(1, 128, 256, 1, 0, 256)
+        first_product(0, 256, 384, 2, 256, 384)
+        first_product(1, 256, 384, 3, 256, 512)
+        first_product(0, 384, 512, 4, 384, 512)
+        first_product(1, 384, 512, 3, 256, 512)
+        first_product(2, 0, 256, 5, 0, 256)
+        first_product(2, 256, 512, 6, 256, 512)
+        first_product(3, 0, 256, 7, 0, 256)
+        first_product(3, 256, 512, 0, 256, 512)
 
         quarters = [slice(q * VQ, (q + 1) * VQ) for q in range(2)]
         t1 = room.tile([P, PACK, V], F32, name="t1", offset=6144, align_bytes=64)
@@ -132,8 +139,8 @@ def tile_picked_csketch_none_p_kernel(tc, x_words, x_scales, w1, sg1, sg2, sg3, 
         def interleave(copy, dst, planes):
             copy(dst.rearrange("p (c i) t -> p c t i", i=LINE), planes.rearrange("p t (c i) -> p c t i", i=LINE))
 
-        def quantize_w2(a):
-            nc.vector.quantize_mx(out=w2_codes[a][:].bitcast(FP8X4), scales=w2_scales[:, a * NH : (a + 1) * NH], in_=w2_bf[a][:].rearrange("p c j -> p (c j)"))
+        def quantize_w2(a, c0, c1):
+            nc.vector.quantize_mx(out=w2_codes[a][:, c0:c1].bitcast(FP8X4), scales=w2_scales[:, a * NH + c0 : a * NH + c1], in_=w2_bf[a][:, c0:c1].rearrange("p c j -> p (c j)"))
 
         def quantize_z(half, c0, c1):
             nc.vector.quantize_mx(
@@ -180,8 +187,10 @@ def tile_picked_csketch_none_p_kernel(tc, x_words, x_scales, w1, sg1, sg2, sg3, 
         z0 = sb.tile([P, PACK, VH], F32, name="z0", align_bytes=64)
         mid1 = sb.tile([P, PACK, VH], F32, name="mid1", align_bytes=64)
 
-        interleave(nc.vector.tensor_copy, w2_bf[0][:], w2_raw[0][:])
-        quantize_w2(0)
+        for c0 in (0, P):
+            interleave(nc.vector.tensor_copy, w2_bf[0][:, c0 : c0 + P], w2_raw[0][:, :, c0 : c0 + P])
+        for c0 in (0, P):
+            quantize_w2(0, c0, c0 + P)
         for t in range(PACK):
             look_up(t1, t, h_sb[0][:], sg1_sb[t // 2][:, t % 2, :])
             turn(diff_ps, t, t1[:, t, VH:], t == 0, False)
@@ -221,7 +230,7 @@ def tile_picked_csketch_none_p_kernel(tc, x_words, x_scales, w1, sg1, sg2, sg3, 
         nc.vector.tensor_tensor(z0[:], mid0[:], hi0[:], MIN)
         interleave(nc.scalar.copy, z_bf[0][:], z0[:])
         nc.vector.tensor_tensor(mid1[:], hi_ps[:], t3[1][:], MIN)
-        quantize_w2(1)
+        quantize_w2(1, 0, NH)
         quantize_z(0, 0, VH)
         second_product(0, 0, 2, 6, nc.scalar.copy, nc.sync)
         second_product(0, 2, 2, 7, nc.scalar.copy, nc.sync)

@@ -110,24 +110,25 @@ def tile_picked_csketch_none_p_kernel(tc, x_words, x_scales, w1, sg1, sg2, sg3, 
             if c1 == b1:
                 nc.scalar.copy(y[t][:, b0:b1], acc[:])
 
-        first_product(0, 0, 128, 0, 0, 256)
-        first_product(1, 0, 128, 1, 0, 256)
-        first_product(0, 128, 256, 0, 0, 256)
-        first_product(1, 128, 256, 1, 0, 256)
-        first_product(0, 256, 384, 2, 256, 384)
-        first_product(1, 256, 384, 3, 256, 512)
-        first_product(0, 384, 512, 4, 384, 512)
-        first_product(1, 384, 512, 3, 256, 512)
-        first_product(2, 0, 256, 5, 0, 256)
-        first_product(2, 256, 512, 6, 256, 512)
-        first_product(3, 0, 256, 7, 0, 256)
-        first_product(3, 256, 512, 0, 256, 512)
+        first_product(0, 0, 128, 0, 0, 128)
+        first_product(1, 0, 128, 1, 0, 128)
+        first_product(0, 128, 256, 2, 128, 256)
+        first_product(1, 128, 256, 3, 128, 256)
+        first_product(0, 256, 384, 4, 256, 384)
+        first_product(1, 256, 384, 5, 256, 512)
+        first_product(0, 384, 512, 6, 384, 512)
+        first_product(1, 384, 512, 5, 256, 512)
+        first_product(2, 0, 256, 7, 0, 256)
+        first_product(2, 256, 512, 0, 256, 512)
+        first_product(3, 0, 256, 1, 0, 256)
+        first_product(3, 256, 512, 2, 256, 512)
 
         quarters = [slice(q * VQ, (q + 1) * VQ) for q in range(2)]
         t1 = room.tile([P, PACK, V], F32, name="t1", offset=6144, align_bytes=64)
         g2 = sb.tile([P, PACK, V], F32, name="g2", align_bytes=64)
         n2 = [sb.tile([P, 2, V], F32, name="n2_0", align_bytes=64), room.tile([P, 2, V], F32, name="n2_1", offset=4096, align_bytes=64)]
-        t3 = [sb.tile([P, PACK, VH], F32, name="t3_0", align_bytes=64), room.tile([P, PACK, VH], F32, name="t3_1", offset=6144, align_bytes=64)]
+        t3 = [sb.tile([P, PACK, VH], F32, name="t3_0", align_bytes=64)]
+        n3 = room.tile([P, 2, VH, 2], F32, name="n3", offset=6144, align_bytes=64)
         g3 = sb.tile([P, PACK, VH], F32, name="g3", align_bytes=64)
         z_bf = [sb.tile([P, VH, PACK], BF16, name="z_bf%d" % half, align_bytes=64) for half in range(2)]
         z_codes = [sb.tile([P, VH], U32, name="z_codes%d" % half, align_bytes=64) for half in range(2)]
@@ -173,19 +174,18 @@ def tile_picked_csketch_none_p_kernel(tc, x_words, x_scales, w1, sg1, sg2, sg3, 
         def turn(acc, t, src, start, stop):
             nc.tensor.matmul(acc[:, t, :], src, ident[:], start=start, stop=stop, is_transpose=True)
 
-        t1_ps = ps.tile([P, PACK, P], F32, name="t1_ps", tag="bank1")
+        t1_ps = ps.tile([P, PACK, P], F32, name="t1_ps", tag="bank4")
         diff_ps = ps.tile([P, PACK, P], F32, name="diff_ps", tag="bank3")
-        n2_ps = ps.tile([P, PACK, P], F32, name="n2_ps", tag="bank4")
-        hi_ps = ps.tile([P, PACK, VH], F32, name="hi_ps", tag="bank2")
-        nlo_ps = ps.tile([P, PACK, VH], F32, name="nlo_ps", tag="bank5")
+        n2_ps = ps.tile([P, PACK, P], F32, name="n2_ps", tag="bank5")
+        hi_ps = ps.tile([P, PACK, VH], F32, name="hi_ps", tag="bank6")
+        nlo_ps = ps.tile([P, PACK, VH], F32, name="nlo_ps", tag="bank7")
         t1_turned = sb.tile([P, PACK, P], F32, name="t1_turned", align_bytes=64)
         n2_turned = sb.tile([P, PACK, P], F32, name="n2_turned", align_bytes=64)
         gap = sb.tile([P, PACK, P], F32, name="gap", align_bytes=64)
-        lo0 = sb.tile([P, PACK, VH], F32, name="lo0", align_bytes=64)
-        hi0 = sb.tile([P, PACK, VH], F32, name="hi0", align_bytes=64)
-        mid0 = sb.tile([P, PACK, VH], F32, name="mid0", align_bytes=64)
-        z0 = sb.tile([P, PACK, VH], F32, name="z0", align_bytes=64)
-        mid1 = sb.tile([P, PACK, VH], F32, name="mid1", align_bytes=64)
+        lo0 = sb.tile([P, 2, VH, 2], F32, name="lo0", align_bytes=64)
+        hi0 = sb.tile([P, 2, VH, 2], F32, name="hi0", align_bytes=64)
+        mid0 = sb.tile([P, 2, VH, 2], F32, name="mid0", align_bytes=64)
+        mid1 = sb.tile([P, 2, VH, 2], F32, name="mid1", align_bytes=64)
 
         for c0 in (0, P):
             interleave(nc.vector.tensor_copy, w2_bf[0][:, c0 : c0 + P], w2_raw[0][:, :, c0 : c0 + P])
@@ -221,25 +221,46 @@ def tile_picked_csketch_none_p_kernel(tc, x_words, x_scales, w1, sg1, sg2, sg3, 
         for t in range(PACK):
             turn(nlo_ps, t, n2_turned[:, t, :], False, t == PACK - 1)
 
+        def paired(planes):
+            return planes.rearrange("p e v -> p v e")
+
+        def by_key(pairs):
+            return pairs.rearrange("p a v e -> p v a e")
+
         for pair in range(2):
             planes = slice(2 * pair, 2 * pair + 2)
-            nc.vector.scalar_tensor_tensor(lo0[:, planes], n2[pair][:, :, :VH], -1.0, t1[:, planes, :VH], MULT, MIN)
-            nc.vector.scalar_tensor_tensor(hi0[:, planes], n2[pair][:, :, :VH], -1.0, t1[:, planes, :VH], MULT, MAX)
-        nc.vector.tensor_tensor(mid0[:], t3[0][:], lo0[:], MAX)
-        nc.vector.tensor_tensor(t3[1][:], g3[:], sg3_sb[:, :, VH:], MULT)
-        nc.vector.tensor_tensor(z0[:], mid0[:], hi0[:], MIN)
-        interleave(nc.scalar.copy, z_bf[0][:], z0[:])
-        nc.vector.tensor_tensor(mid1[:], hi_ps[:], t3[1][:], MIN)
-        quantize_w2(1, 0, NH)
+            nc.vector.scalar_tensor_tensor(lo0[:, pair], paired(n2[pair][:, :, :VH]), -1.0, paired(t1[:, planes, :VH]), MULT, MIN)
+            nc.vector.scalar_tensor_tensor(hi0[:, pair], paired(n2[pair][:, :, :VH]), -1.0, paired(t1[:, planes, :VH]), MULT, MAX)
+        nc.vector.tensor_tensor(mid0[:], t3[0][:].rearrange("p (a e) v -> p a v e", e=2), lo0[:], MAX)
+        for pair in range(2):
+            planes = slice(2 * pair, 2 * pair + 2)
+            nc.vector.scalar_tensor_tensor(n3[:, pair], paired(g3[:, planes]), -1.0, paired(sg3_sb[:, planes, VH:]), MULT, MULT)
+        nc.vector.tensor_tensor(z_bf[0][:].rearrange("p v (a e) -> p v a e", e=2), by_key(mid0[:]), by_key(hi0[:]), MIN)
+        for pair in range(2):
+            planes = slice(2 * pair, 2 * pair + 2)
+            nc.vector.scalar_tensor_tensor(mid1[:, pair], paired(hi_ps[:, planes]), -1.0, n3[:, pair], MULT, MAX)
         quantize_z(0, 0, VH)
-        second_product(0, 0, 2, 6, nc.scalar.copy, nc.sync)
-        second_product(0, 2, 2, 7, nc.scalar.copy, nc.sync)
+        second_product(0, 0, 2, 0, nc.scalar.copy, nc.sync)
+        quantize_w2(1, 0, NH)
+        second_product(0, 2, 2, 1, nc.scalar.copy, nc.sync)
         for keys in quarters:
-            nc.vector.scalar_tensor_tensor(z_bf[1][:, keys], nlo_ps[:, :, keys].rearrange("p t v -> p v t"), -1.0, mid1[:, :, keys].rearrange("p t v -> p v t"), MULT, MAX)
+            nc.vector.tensor_tensor(
+                z_bf[1][:, keys].rearrange("p v (a e) -> p v a e", e=2),
+                nlo_ps[:, :, keys].rearrange("p (a e) v -> p v a e", e=2),
+                by_key(mid1[:, :, keys]),
+                MIN,
+            )
         for keys in quarters:
             quantize_z(1, keys.start, keys.stop)
+
+        def negate_on_scalar(dst, src):
+            nc.scalar.activation(dst, src, COPY, scale=-1.0)
+
+        def negate_on_vector(dst, src):
+            nc.vector.tensor_scalar_mul(dst, src, -1.0)
+
         for u in range(PACK):
             if u % 2 == 0:
-                second_product(1, u, 1, (1, 3, 4, 0)[u], nc.scalar.copy, nc.scalar)
+                second_product(1, u, 1, (2, 3, 4, 5)[u], negate_on_scalar, nc.scalar)
             else:
-                second_product(1, u, 1, (1, 3, 4, 0)[u], nc.vector.tensor_copy, nc.sync)
+                second_product(1, u, 1, (2, 3, 4, 5)[u], negate_on_vector, nc.sync)

@@ -175,10 +175,10 @@ def tile_picked_csketch_none_p_kernel(tc, x_words, x_scales, w1, sg1, sg2, sg3, 
             nc.tensor.matmul(acc[:, t, :], src, ident[:], start=start, stop=stop, is_transpose=True)
 
         t1_ps = ps.tile([P, PACK, P], F32, name="t1_ps", tag="bank4")
-        diff_ps = ps.tile([P, PACK, P], F32, name="diff_ps", tag="bank3")
-        n2_ps = ps.tile([P, PACK, P], F32, name="n2_ps", tag="bank5")
-        hi_ps = ps.tile([P, PACK, VH], F32, name="hi_ps", tag="bank6")
-        nlo_ps = ps.tile([P, PACK, VH], F32, name="nlo_ps", tag="bank7")
+        diff_ps = [ps.tile([P, 2, P], F32, name="diff_ps%d" % pair, tag="bank%d" % (3, 6)[pair]) for pair in range(2)]
+        n2_ps = [ps.tile([P, 2, P], F32, name="n2_ps%d" % pair, tag="bank%d" % (5, 7)[pair]) for pair in range(2)]
+        hi_ps = ps.tile([P, PACK, VH], F32, name="hi_ps", tag="bank0")
+        nlo_ps = ps.tile([P, PACK, VH], F32, name="nlo_ps", tag="bank1")
         t1_turned = sb.tile([P, PACK, P], F32, name="t1_turned", align_bytes=64)
         n2_turned = sb.tile([P, PACK, P], F32, name="n2_turned", align_bytes=64)
         gap = sb.tile([P, PACK, P], F32, name="gap", align_bytes=64)
@@ -193,7 +193,7 @@ def tile_picked_csketch_none_p_kernel(tc, x_words, x_scales, w1, sg1, sg2, sg3, 
             quantize_w2(0, c0, c0 + P)
         for t in range(PACK):
             look_up(t1, t, h_sb[0][:], sg1_sb[t // 2][:, t % 2, :])
-            turn(diff_ps, t, t1[:, t, VH:], t == 0, False)
+            turn(diff_ps[t // 2], t % 2, t1[:, t, VH:], t % 2 == 0, False)
             turn(t1_ps, t, t1[:, t, VH:], t == 0, t == PACK - 1)
         for t in range(PACK):
             nc.scalar.activation(g2[:, t, :], y[t][:].indirect(h_sb[1][:]), COPY)
@@ -206,20 +206,23 @@ def tile_picked_csketch_none_p_kernel(tc, x_words, x_scales, w1, sg1, sg2, sg3, 
                 look_up(t3[0], t, h_sb[2][:, : VH // 16], sg3_sb[:, t, :VH])
             nc.vector.scalar_tensor_tensor(n2[pair][:], g2[:, planes], -1.0, sg2_sb[:, planes], MULT, MULT)
             for t in range(2 * pair, 2 * pair + 2):
-                turn(diff_ps, t, n2[pair][:, t % 2, VH:], False, t == PACK - 1)
+                turn(diff_ps[pair], t % 2, n2[pair][:, t % 2, VH:], False, t % 2 == 1)
             for t in range(2 * pair, 2 * pair + 2):
-                turn(n2_ps, t, n2[pair][:, t % 2, VH:], t == 0, t == PACK - 1)
+                turn(n2_ps[pair], t % 2, n2[pair][:, t % 2, VH:], t % 2 == 0, t % 2 == 1)
         for t in range(PACK):
             turn(hi_ps, t, t1_turned[:, t, :], t == 0, False)
-        nc.scalar.activation(gap[:], diff_ps[:], RELU, scale=-1.0)
-        nc.scalar.copy(n2_turned[:], n2_ps[:])
+        for pair in range(2):
+            planes = slice(2 * pair, 2 * pair + 2)
+            nc.scalar.activation(gap[:, planes], diff_ps[pair][:], RELU, scale=-1.0)
+            nc.scalar.copy(n2_turned[:, planes], n2_ps[pair][:])
         interleave(nc.scalar.copy, w2_bf[1][:], w2_raw[1][:])
         for t in range(PACK):
             turn(hi_ps, t, gap[:, t, :], False, t == PACK - 1)
-        for t in range(PACK):
-            turn(nlo_ps, t, gap[:, t, :], t == 0, False)
-        for t in range(PACK):
-            turn(nlo_ps, t, n2_turned[:, t, :], False, t == PACK - 1)
+        for pair in range(2):
+            for t in range(2 * pair, 2 * pair + 2):
+                turn(nlo_ps, t, gap[:, t, :], t == 0, False)
+            for t in range(2 * pair, 2 * pair + 2):
+                turn(nlo_ps, t, n2_turned[:, t, :], False, t == PACK - 1)
 
         def paired(planes):
             return planes.rearrange("p e v -> p v e")
@@ -240,9 +243,9 @@ def tile_picked_csketch_none_p_kernel(tc, x_words, x_scales, w1, sg1, sg2, sg3, 
             planes = slice(2 * pair, 2 * pair + 2)
             nc.vector.scalar_tensor_tensor(mid1[:, pair], paired(hi_ps[:, planes]), -1.0, n3[:, pair], MULT, MAX)
         quantize_z(0, 0, VH)
-        second_product(0, 0, 2, 0, nc.scalar.copy, nc.sync)
+        second_product(0, 0, 2, 2, nc.scalar.copy, nc.sync)
         quantize_w2(1, 0, NH)
-        second_product(0, 2, 2, 1, nc.scalar.copy, nc.sync)
+        second_product(0, 2, 2, 4, nc.scalar.copy, nc.sync)
         for keys in quarters:
             nc.vector.tensor_tensor(
                 z_bf[1][:, keys].rearrange("p v (a e) -> p v a e", e=2),
@@ -261,6 +264,6 @@ def tile_picked_csketch_none_p_kernel(tc, x_words, x_scales, w1, sg1, sg2, sg3, 
 
         for u in range(PACK):
             if u % 2 == 0:
-                second_product(1, u, 1, (2, 3, 4, 5)[u], negate_on_scalar, nc.scalar)
+                second_product(1, u, 1, (3, 6, 5, 7)[u], negate_on_scalar, nc.scalar)
             else:
-                second_product(1, u, 1, (2, 3, 4, 5)[u], negate_on_vector, nc.sync)
+                second_product(1, u, 1, (3, 6, 5, 7)[u], negate_on_vector, nc.sync)

@@ -36,15 +36,15 @@ def tile_picked_csketch_none_p_kernel(tc, x_words, x_scales, w1, sg1, sg2, sg3, 
 
         offs_sb = sb.tile([P, S // 16], U16, name="offs_sb")
         h_sb = [sb.tile([P, V // 16], U16, name="h%d_sb" % n) for n in range(3)]
-        xw = sb.tile([P, T], U32, name="xw", align_bytes=64)
-        xs = sb.tile([P, T], U8, name="xs", align_bytes=64)
-        w1_raw = sb.tile([P, PACK, H], F32, name="w1_raw", align_bytes=64)
-        w2_raw = [sb.tile([P, PACK, NH], F32, name="w2_raw%d" % a, align_bytes=64) for a in range(2)]
+        xw = sb.tile([P, T], U32, name="xw", align_bytes=256)
+        xs = sb.tile([P, T], U8, name="xs", align_bytes=256)
+        w1_raw = sb.tile([P, PACK, H], F32, name="w1_raw", align_bytes=256)
+        w2_raw = [sb.tile([P, PACK, NH], F32, name="w2_raw%d" % a, align_bytes=256) for a in range(2)]
         w2_rows = w2.rearrange("(p j) c -> p j c", j=PACK)
         room = ctx.enter_context(tc.tile_pool(name="room", bufs=1))
-        sg1_sb = [room.tile([P, 2, V], F32, name="sg1_%d" % pair, offset=pair * 2 * V * 4, align_bytes=64) for pair in range(2)]
-        sg2_sb = sb.tile([P, PACK, V], F32, name="sg2_sb", align_bytes=64)
-        sg3_sb = sb.tile([P, PACK, V], F32, name="sg3_sb", align_bytes=64)
+        sg1_sb = [room.tile([P, 2, V], F32, name="sg1_%d" % pair, offset=pair * 2 * V * 4, align_bytes=256) for pair in range(2)]
+        sg2_sb = sb.tile([P, PACK, V], F32, name="sg2_sb", align_bytes=256)
+        sg3_sb = sb.tile([P, PACK, V], F32, name="sg3_sb", align_bytes=256)
         ident = sb.tile([P, P], F32, name="ident", align_bytes=64)
         make_identity(nc, ident[:])
         sg_planes = [sg.rearrange("(p t) v -> p t v", t=PACK) for sg in (sg1, sg2, sg3)]
@@ -164,7 +164,7 @@ def tile_picked_csketch_none_p_kernel(tc, x_words, x_scales, w1, sg1, sg2, sg3, 
                     start=True,
                     stop=True,
                 )
-            res = sb.tile([P, count, VH], F32, name="res%d_%d" % (half, u0), align_bytes=64)
+            res = sb.tile([P, count, VH], F32, name="res%d_%d" % (half, u0), align_bytes=256)
             copy_engine(res[:], acc[:])
             store_engine.dma_start(out_rows[:, u0 : u0 + count, half * VH : (half + 1) * VH], res[:])
 

@@ -22,7 +22,7 @@ RELU = mybir.ActivationFunctionType.Relu
 P = 128
 PACK = 4
 LINE = 4
-W1_VECTOR_ROWS = 48
+W1_VECTOR_ROWS = 72
 VH = V // 2
 VQ = V // 4
 NH = N // 2
@@ -37,41 +37,44 @@ def tile_picked_csketch_none_p_kernel(tc, x_words, x_scales, w1, sg1, sg2, sg3, 
         offs_sb = sb.tile([P, S // 16], U16, name="offs_sb")
         h_sb = [sb.tile([P, V // 16], U16, name="h%d_sb" % n) for n in range(3)]
         xw = sb.tile([P, T], U32, name="xw", align_bytes=256)
-        xs = sb.tile([P, T], U8, name="xs", align_bytes=256)
-        w1_raw = sb.tile([P, PACK, H], F32, name="w1_raw", align_bytes=256)
-        w2_raw = [sb.tile([P, PACK, NH], F32, name="w2_raw%d" % a, align_bytes=256) for a in range(2)]
-        w2_rows = w2.rearrange("(p j) c -> p j c", j=PACK)
         room = ctx.enter_context(tc.tile_pool(name="room", bufs=1))
-        sg1_sb = [room.tile([P, 2, V], F32, name="sg1_%d" % pair, offset=pair * 2 * V * 4, align_bytes=256) for pair in range(2)]
-        sg2_sb = sb.tile([P, PACK, V], F32, name="sg2_sb", align_bytes=256)
-        sg3_sb = sb.tile([P, PACK, V], F32, name="sg3_sb", align_bytes=256)
+        head = ctx.enter_context(tc.tile_pool(name="head", bufs=1))
+        xs = head.tile([P, T], U8, name="xs", offset=3072, align_bytes=256)
+        w1_raw = head.tile([P, PACK, H], F32, name="w1_raw", offset=6144, align_bytes=256)
+        w1_bf = head.tile([P, PACK, P, PACK], BF16, name="w1_bf", offset=16384, align_bytes=256)
+        w2_raw = [head.tile([P, PACK, NH], F32, name="w2_raw%d" % a, offset=(0, 18432)[a], align_bytes=256) for a in range(2)]
+        sg1_sb = [head.tile([P, 2, V], F32, name="sg1_%d" % pair, offset=(4096, 6144)[pair], align_bytes=256) for pair in range(2)]
+        sg3_sb = head.tile([P, PACK, V], F32, name="sg3_sb", offset=8192, align_bytes=256)
+        sg2_sb = head.tile([P, PACK, V], F32, name="sg2_sb", offset=14336, align_bytes=256)
+        w2_rows = w2.rearrange("(p j) c -> p j c", j=PACK)
         ident = sb.tile([P, P], F32, name="ident", align_bytes=64)
         make_identity(nc, ident[:])
         sg_planes = [sg.rearrange("(p t) v -> p t v", t=PACK) for sg in (sg1, sg2, sg3)]
+        w1_rows = w1.rearrange("(p j) c -> p j c", j=PACK)
         nc.vector.memset(xs[:].bitcast(I32), 0)
-        nc.sync.dma_start(w1_raw[:], w1.rearrange("(p j) c -> p j c", j=PACK))
+        nc.sync.dma_start(w1_raw[:, :2], w1_rows[:, :2])
         nc.sync.dma_start(offs_sb[:], offs)
-        for q in range(4):
-            nc.sync.dma_start(xs[q:P:32, :].bitcast(I32), x_scales[0, q:16:4, :].bitcast(I32))
+        nc.sync.dma_start(xs[0:P:8, :].bitcast(I32), x_scales[0].bitcast(I32))
+        nc.sync.dma_start(w1_raw[:, 2:], w1_rows[:, 2:])
         nc.sync.dma_start(xw[:].bitcast(I32), x_words[0].rearrange("p n t -> p (n t)").bitcast(I32))
-        nc.sync.dma_start(w2_raw[0][:], w2_rows[:, :, :NH])
-        nc.sync.dma_start(sg1_sb[0][:], sg_planes[0][:, :2])
         nc.sync.dma_start(h_sb[0][:], h1)
-        nc.sync.dma_start(sg1_sb[1][:], sg_planes[0][:, 2:])
         nc.sync.dma_start(h_sb[1][:], h2)
         nc.sync.dma_start(h_sb[2][:], h3)
-        nc.sync.dma_start(sg3_sb[:], sg_planes[2])
-        nc.sync.dma_start(sg2_sb[:], sg_planes[1])
-        nc.sync.dma_start(w2_raw[1][:], w2_rows[:, :, NH:])
 
-        gs = sb.tile([P, S], U8, name="gs", align_bytes=64)
-        nc.vector.tensor_copy(gs[:], xs[:].indirect(offs_sb[:]))
+        gs_spread = sb.tile([P, S], U8, name="gs_spread", align_bytes=256)
+        gs = sb.tile([P, S], U8, name="gs", align_bytes=256)
+        nc.vector.tensor_copy(gs_spread[:], xs[:].indirect(offs_sb[:]))
+        nc.vector.tensor_copy(gs[:].bitcast(I32), gs_spread[:].bitcast(I32))
+        for q in range(1, 4):
+            nc.sync.dma_start(gs[q:P:32, :].bitcast(I32), gs_spread[8 * q : P : 32, :].bitcast(I32))
+        nc.sync.dma_start(w2_raw[0][:], w2_rows[:, :, :NH])
+        nc.sync.dma_start(sg1_sb[0][:], sg_planes[0][:, :2])
 
-        w1_bf = sb.tile([P, PACK, P, PACK], BF16, name="w1_bf", align_bytes=64)
         src = w1_raw[:].rearrange("p j (m t) -> p m j t", t=PACK)
         dst = w1_bf[:].rearrange("p t m j -> p m j t")
         nc.vector.tensor_copy(dst[:, :W1_VECTOR_ROWS], src[:, :W1_VECTOR_ROWS])
-        nc.scalar.copy(dst[:, W1_VECTOR_ROWS:], src[:, W1_VECTOR_ROWS:])
+        for j in (0, 2):
+            nc.scalar.copy(dst[:, W1_VECTOR_ROWS:, j : j + 2], src[:, W1_VECTOR_ROWS:, j : j + 2])
         w1_codes = sb.tile([P, H], U32, name="w1_codes", align_bytes=64)
         w1_scales = sb.tile([P, H], U8, name="w1_scales", align_bytes=64)
 
@@ -83,9 +86,12 @@ def tile_picked_csketch_none_p_kernel(tc, x_words, x_scales, w1, sg1, sg2, sg3, 
                 in_=w1_bf[:, 2 * pair : 2 * pair + 2].rearrange("p t m j -> p (t m j)"),
             )
 
+        nc.sync.dma_start(sg1_sb[1][:], sg_planes[0][:, 2:])
+        nc.sync.dma_start(sg3_sb[:], sg_planes[2])
         quantize_w1(0)
-
         quantize_w1(1)
+        nc.sync.dma_start(sg2_sb[:], sg_planes[1])
+        nc.sync.dma_start(w2_raw[1][:], w2_rows[:, :, NH:])
 
         gw = sb.tile([P, S], U32, name="gw", align_bytes=64)
         for c0 in range(0, S, P):
@@ -129,7 +135,6 @@ def tile_picked_csketch_none_p_kernel(tc, x_words, x_scales, w1, sg1, sg2, sg3, 
         n2 = [sb.tile([P, 2, V], F32, name="n2_0", align_bytes=64), room.tile([P, 2, V], F32, name="n2_1", offset=4096, align_bytes=64)]
         t3 = [sb.tile([P, PACK, VH], F32, name="t3_0", align_bytes=64)]
         n3 = room.tile([P, 2, VH, 2], F32, name="n3", offset=6144, align_bytes=64)
-        g3 = sb.tile([P, PACK, VH], F32, name="g3", align_bytes=64)
         z_bf = [sb.tile([P, VH, PACK], BF16, name="z_bf%d" % half, align_bytes=64) for half in range(2)]
         z_codes = [sb.tile([P, VH], U32, name="z_codes%d" % half, align_bytes=64) for half in range(2)]
         z_scales = [sb.tile([P, VH], U8, name="z_scales%d" % half, align_bytes=64) for half in range(2)]
@@ -198,12 +203,11 @@ def tile_picked_csketch_none_p_kernel(tc, x_words, x_scales, w1, sg1, sg2, sg3, 
         for t in range(PACK):
             nc.scalar.activation(g2[:, t, :], y[t][:].indirect(h_sb[1][:]), COPY)
         nc.scalar.copy(t1_turned[:], t1_ps[:])
-        for t in range(PACK):
-            nc.scalar.activation(g3[:, t, :], y[t][:].indirect(h_sb[2][:, VH // 16 :]), COPY)
         for pair in range(2):
             planes = slice(2 * pair, 2 * pair + 2)
             for t in range(2 * pair, 2 * pair + 2):
                 look_up(t3[0], t, h_sb[2][:, : VH // 16], sg3_sb[:, t, :VH])
+                nc.scalar.activation(sg3_sb[:, t, :VH], y[t][:].indirect(h_sb[2][:, VH // 16 :]), COPY)
             nc.vector.scalar_tensor_tensor(n2[pair][:], g2[:, planes], -1.0, sg2_sb[:, planes], MULT, MULT)
             for t in range(2 * pair, 2 * pair + 2):
                 turn(diff_ps[pair], t % 2, n2[pair][:, t % 2, VH:], False, t % 2 == 1)
@@ -237,7 +241,7 @@ def tile_picked_csketch_none_p_kernel(tc, x_words, x_scales, w1, sg1, sg2, sg3, 
         nc.vector.tensor_tensor(mid0[:], t3[0][:].rearrange("p (a e) v -> p a v e", e=2), lo0[:], MAX)
         for pair in range(2):
             planes = slice(2 * pair, 2 * pair + 2)
-            nc.vector.scalar_tensor_tensor(n3[:, pair], paired(g3[:, planes]), -1.0, paired(sg3_sb[:, planes, VH:]), MULT, MULT)
+            nc.vector.scalar_tensor_tensor(n3[:, pair], paired(sg3_sb[:, planes, :VH]), -1.0, paired(sg3_sb[:, planes, VH:]), MULT, MULT)
         nc.vector.tensor_tensor(z_bf[0][:].rearrange("p v (a e) -> p v a e", e=2), by_key(mid0[:]), by_key(hi0[:]), MIN)
         for pair in range(2):
             planes = slice(2 * pair, 2 * pair + 2)

from contextlib import ExitStack

import concourse.mybir as mybir
from concourse.masks import make_identity

K, T, S, V, N, H = 512, 2048, 512, 256, 512, 512
FLOPS = 2 * K * H * S + 2 * H * N * V

F32 = mybir.dt.float32
BF16 = mybir.dt.bfloat16
I32 = mybir.dt.int32
U32 = mybir.dt.uint32
U16 = mybir.dt.uint16
U8 = mybir.dt.uint8
FP8X4 = mybir.dt.float8_e4m3fn_x4
MULT = mybir.AluOpType.mult
MIN = mybir.AluOpType.min
MAX = mybir.AluOpType.max
COPY = mybir.ActivationFunctionType.Copy
RELU = mybir.ActivationFunctionType.Relu

P = 128
PACK = 4
LINE = 4
W1_VECTOR_ROWS = 72
VH = V // 2
VQ = V // 4
NH = N // 2


def tile_picked_csketch_none_p_kernel(tc, x_words, x_scales, w1, sg1, sg2, sg3, w2, offs, h1, h2, h3, out):
    nc = tc.nc
    with ExitStack() as ctx:
        sb = ctx.enter_context(tc.tile_pool(name="sb", bufs=1))
        ps = ctx.enter_context(tc.psum_pool(name="ps", bufs=1))

        offs_sb = sb.tile([P, S // 16], U16, name="offs_sb")
        h_sb = [sb.tile([P, V // 16], U16, name="h%d_sb" % n) for n in range(3)]
        xw = sb.tile([P, T], U32, name="xw", align_bytes=256)
        room = ctx.enter_context(tc.tile_pool(name="room", bufs=1))
        head = ctx.enter_context(tc.tile_pool(name="head", bufs=1))
        xs = head.tile([P, T], U8, name="xs", offset=3072, align_bytes=256)
        w1_raw = head.tile([P, PACK, H], F32, name="w1_raw", offset=6144, align_bytes=256)
        w1_bf = head.tile([P, PACK, P, PACK], BF16, name="w1_bf", offset=16384, align_bytes=256)
        w2_raw = [head.tile([P, PACK, NH], F32, name="w2_raw%d" % a, offset=(0, 18432)[a], align_bytes=256) for a in range(2)]
        sg1_sb = [head.tile([P, 2, V], F32, name="sg1_%d" % pair, offset=(4096, 6144)[pair], align_bytes=256) for pair in range(2)]
        sg3_sb = head.tile([P, PACK, V], F32, name="sg3_sb", offset=8192, align_bytes=256)
        sg2_sb = head.tile([P, PACK, V], F32, name="sg2_sb", offset=14336, align_bytes=256)
        w2_rows = w2.rearrange("(p j) c -> p j c", j=PACK)
        ident = sb.tile([P, P], F32, name="ident", align_bytes=64)
        make_identity(nc, ident[:])
        sg_planes = [sg.rearrange("(p t) v -> p t v", t=PACK) for sg in (sg1, sg2, sg3)]
        w1_rows = w1.rearrange("(p j) c -> p j c", j=PACK)
        nc.vector.memset(xs[:].bitcast(I32), 0)
        nc.sync.dma_start(w1_raw[:, :2], w1_rows[:, :2])
        nc.sync.dma_start(offs_sb[:], offs)
        nc.sync.dma_start(xs[0:P:8, :].bitcast(I32), x_scales[0].bitcast(I32))
        nc.sync.dma_start(w1_raw[:, 2:], w1_rows[:, 2:])
        nc.sync.dma_start(xw[:].bitcast(I32), x_words[0].rearrange("p n t -> p (n t)").bitcast(I32))
        nc.sync.dma_start(h_sb[0][:], h1)
        nc.sync.dma_start(h_sb[1][:], h2)
        nc.sync.dma_start(h_sb[2][:], h3)

        gs_spread = sb.tile([P, S], U8, name="gs_spread", align_bytes=256)
        gs = sb.tile([P, S], U8, name="gs", align_bytes=256)
        nc.vector.tensor_copy(gs_spread[:], xs[:].indirect(offs_sb[:]))
        nc.vector.tensor_copy(gs[:].bitcast(I32), gs_spread[:].bitcast(I32))
        for q in range(1, 4):
            nc.sync.dma_start(gs[q:P:32, :].bitcast(I32), gs_spread[8 * q : P : 32, :].bitcast(I32))
        nc.sync.dma_start(w2_raw[0][:], w2_rows[:, :, :NH])
        nc.sync.dma_start(sg1_sb[0][:], sg_planes[0][:, :2])

        src = w1_raw[:].rearrange("p j (m t) -> p m j t", t=PACK)
        dst = w1_bf[:].rearrange("p t m j -> p m j t")
        nc.vector.tensor_copy(dst[:, :W1_VECTOR_ROWS], src[:, :W1_VECTOR_ROWS])
        for j in (0, 2):
            nc.scalar.copy(dst[:, W1_VECTOR_ROWS:, j : j + 2], src[:, W1_VECTOR_ROWS:, j : j + 2])
        w1_codes = sb.tile([P, H], U32, name="w1_codes", align_bytes=64)
        w1_scales = sb.tile([P, H], U8, name="w1_scales", align_bytes=64)

        def quantize_w1(pair):
            cols = slice(2 * pair * P, 2 * (pair + 1) * P)
            nc.vector.quantize_mx(
                out=w1_codes[:, cols].bitcast(FP8X4),
                scales=w1_scales[:, cols],
                in_=w1_bf[:, 2 * pair : 2 * pair + 2].rearrange("p t m j -> p (t m j)"),
            )

        nc.sync.dma_start(sg1_sb[1][:], sg_planes[0][:, 2:])
        nc.sync.dma_start(sg3_sb[:], sg_planes[2])
        quantize_w1(0)
        quantize_w1(1)
        nc.sync.dma_start(sg2_sb[:], sg_planes[1])
        nc.sync.dma_start(w2_raw[1][:], w2_rows[:, :, NH:])

        gw = sb.tile([P, S], U32, name="gw", align_bytes=64)
        for c0 in range(0, S, P):
            nc.vector.tensor_copy(gw[:, c0 : c0 + P], xw[:].indirect(offs_sb[:, c0 // 16 : (c0 + P) // 16]))

        y = [sb.tile([P, S], F32, name="y%d" % t, align_bytes=64) for t in range(PACK)]
        banks = {}

        def first_product(t, c0, c1, bank, b0, b1):
            if c0 == b0:
                banks[bank] = ps.tile([P, b1 - b0], F32, name="y_ps%d_%d" % (t, b0), tag="bank%d" % bank)
            acc = banks[bank]
            nc.tensor.matmul_mx(
                out=acc[:, c0 - b0 : c1 - b0],
                lhsT=w1_codes[:, t * P : (t + 1) * P].bitcast(FP8X4),
                lhsT_scale=w1_scales[:, t * P : (t + 1) * P],
                rhs=gw[:, c0:c1].bitcast(FP8X4),
                rhs_scale=gs[:, c0:c1],
                start=True,
                stop=True,
            )
            if c1 == b1:
                nc.scalar.copy(y[t][:, b0:b1], acc[:])

        first_product(0, 0, 128, 0, 0, 128)
        first_product(1, 0, 128, 1, 0, 128)
        first_product(0, 128, 256, 2, 128, 256)
        first_product(1, 128, 256, 3, 128, 256)
        first_product(0, 256, 384, 4, 256, 384)
        first_product(1, 256, 384, 5, 256, 512)
        first_product(0, 384, 512, 6, 384, 512)
        first_product(1, 384, 512, 5, 256, 512)
        first_product(2, 0, 256, 7, 0, 256)
        first_product(2, 256, 512, 0, 256, 512)
        first_product(3, 0, 256, 1, 0, 256)
        first_product(3, 256, 512, 2, 256, 512)

        quarters = [slice(q * VQ, (q + 1) * VQ) for q in range(2)]
        t1 = room.tile([P, PACK, V], F32, name="t1", offset=6144, align_bytes=64)
        g2 = sb.tile([P, PACK, V], F32, name="g2", align_bytes=64)
        n2 = [sb.tile([P, 2, V], F32, name="n2_0", align_bytes=64), room.tile([P, 2, V], F32, name="n2_1", offset=4096, align_bytes=64)]
        t3 = [sb.tile([P, PACK, VH], F32, name="t3_0", align_bytes=64)]
        n3 = room.tile([P, 2, VH, 2], F32, name="n3", offset=6144, align_bytes=64)
        z_bf = [sb.tile([P, VH, PACK], BF16, name="z_bf%d" % half, align_bytes=64) for half in range(2)]
        z_codes = [sb.tile([P, VH], U32, name="z_codes%d" % half, align_bytes=64) for half in range(2)]
        z_scales = [sb.tile([P, VH], U8, name="z_scales%d" % half, align_bytes=64) for half in range(2)]
        w2_bf = [sb.tile([P, NH, PACK], BF16, name="w2_bf0", align_bytes=64), room.tile([P, NH, PACK], BF16, name="w2_bf1", offset=4096, align_bytes=64)]
        w2_codes = [sb.tile([P, NH], U32, name="w2_codes%d" % a, align_bytes=64) for a in range(2)]
        w2_scales = sb.tile([P, N], U8, name="w2_scales", align_bytes=64)

        def interleave(copy, dst, planes):
            copy(dst.rearrange("p (c i) t -> p c t i", i=LINE), planes.rearrange("p t (c i) -> p c t i", i=LINE))

        def quantize_w2(a, c0, c1):
            nc.vector.quantize_mx(out=w2_codes[a][:, c0:c1].bitcast(FP8X4), scales=w2_scales[:, a * NH + c0 : a * NH + c1], in_=w2_bf[a][:, c0:c1].rearrange("p c j -> p (c j)"))

        def quantize_z(half, c0, c1):
            nc.vector.quantize_mx(
                out=z_codes[half][:, c0:c1].bitcast(FP8X4),
                scales=z_scales[half][:, c0:c1],
                in_=z_bf[half][:, c0:c1, :].rearrange("p v t -> p (v t)"),
            )

        out_rows = out.rearrange("(u p) v -> p u v", p=P)

        def second_product(half, u0, count, bank, copy_engine, store_engine):
            acc = ps.tile([P, count, VH], F32, name="o_ps%d_%d" % (half, u0), tag="bank%d" % bank)
            for u in range(u0, u0 + count):
                nc.tensor.matmul_mx(
                    out=acc[:, u - u0, :],
                    lhsT=w2_codes[u // 2][:, u % 2 * P : (u % 2 + 1) * P].bitcast(FP8X4),
                    lhsT_scale=w2_scales[:, u * P : (u + 1) * P],
                    rhs=z_codes[half][:].bitcast(FP8X4),
                    rhs_scale=z_scales[half][:],
                    start=True,
                    stop=True,
                )
            res = sb.tile([P, count, VH], F32, name="res%d_%d" % (half, u0), align_bytes=256)
            copy_engine(res[:], acc[:])
            store_engine.dma_start(out_rows[:, u0 : u0 + count, half * VH : (half + 1) * VH], res[:])

        def look_up(dst, t, offsets, signs):
            nc.vector.tensor_tensor(dst[:, t, :], y[t][:].indirect(offsets), signs, MULT)

        def turn(acc, t, src, start, stop):
            nc.tensor.matmul(acc[:, t, :], src, ident[:], start=start, stop=stop, is_transpose=True)

        t1_ps = ps.tile([P, PACK, P], F32, name="t1_ps", tag="bank4")
        diff_ps = [ps.tile([P, 2, P], F32, name="diff_ps%d" % pair, tag="bank%d" % (3, 6)[pair]) for pair in range(2)]
        n2_ps = [ps.tile([P, 2, P], F32, name="n2_ps%d" % pair, tag="bank%d" % (5, 7)[pair]) for pair in range(2)]
        hi_ps = ps.tile([P, PACK, VH], F32, name="hi_ps", tag="bank0")
        nlo_ps = ps.tile([P, PACK, VH], F32, name="nlo_ps", tag="bank1")
        t1_turned = sb.tile([P, PACK, P], F32, name="t1_turned", align_bytes=64)
        n2_turned = sb.tile([P, PACK, P], F32, name="n2_turned", align_bytes=64)
        gap = sb.tile([P, PACK, P], F32, name="gap", align_bytes=64)
        lo0 = sb.tile([P, 2, VH, 2], F32, name="lo0", align_bytes=64)
        hi0 = sb.tile([P, 2, VH, 2], F32, name="hi0", align_bytes=64)
        mid0 = sb.tile([P, 2, VH, 2], F32, name="mid0", align_bytes=64)
        mid1 = sb.tile([P, 2, VH, 2], F32, name="mid1", align_bytes=64)

        for c0 in (0, P):
            interleave(nc.vector.tensor_copy, w2_bf[0][:, c0 : c0 + P], w2_raw[0][:, :, c0 : c0 + P])
        for c0 in (0, P):
            quantize_w2(0, c0, c0 + P)
        for t in range(PACK):
            look_up(t1, t, h_sb[0][:], sg1_sb[t // 2][:, t % 2, :])
            turn(diff_ps[t // 2], t % 2, t1[:, t, VH:], t % 2 == 0, False)
            turn(t1_ps, t, t1[:, t, VH:], t == 0, t == PACK - 1)
        for t in range(PACK):
            nc.scalar.activation(g2[:, t, :], y[t][:].indirect(h_sb[1][:]), COPY)
        nc.scalar.copy(t1_turned[:], t1_ps[:])
        for pair in range(2):
            planes = slice(2 * pair, 2 * pair + 2)
            for t in range(2 * pair, 2 * pair + 2):
                look_up(t3[0], t, h_sb[2][:, : VH // 16], sg3_sb[:, t, :VH])
                nc.scalar.activation(sg3_sb[:, t, :VH], y[t][:].indirect(h_sb[2][:, VH // 16 :]), COPY)
            nc.vector.scalar_tensor_tensor(n2[pair][:], g2[:, planes], -1.0, sg2_sb[:, planes], MULT, MULT)
            for t in range(2 * pair, 2 * pair + 2):
                turn(diff_ps[pair], t % 2, n2[pair][:, t % 2, VH:], False, t % 2 == 1)
            for t in range(2 * pair, 2 * pair + 2):
                turn(n2_ps[pair], t % 2, n2[pair][:, t % 2, VH:], t % 2 == 0, t % 2 == 1)
        for t in range(PACK):
            turn(hi_ps, t, t1_turned[:, t, :], t == 0, False)
        for pair in range(2):
            planes = slice(2 * pair, 2 * pair + 2)
            nc.scalar.activation(gap[:, planes], diff_ps[pair][:], RELU, scale=-1.0)
            nc.scalar.copy(n2_turned[:, planes], n2_ps[pair][:])
        interleave(nc.scalar.copy, w2_bf[1][:], w2_raw[1][:])
        for t in range(PACK):
            turn(hi_ps, t, gap[:, t, :], False, t == PACK - 1)
        for pair in range(2):
            for t in range(2 * pair, 2 * pair + 2):
                turn(nlo_ps, t, gap[:, t, :], t == 0, False)
            for t in range(2 * pair, 2 * pair + 2):
                turn(nlo_ps, t, n2_turned[:, t, :], False, t == PACK - 1)

        def paired(planes):
            return planes.rearrange("p e v -> p v e")

        def by_key(pairs):
            return pairs.rearrange("p a v e -> p v a e")

        for pair in range(2):
            planes = slice(2 * pair, 2 * pair + 2)
            nc.vector.scalar_tensor_tensor(lo0[:, pair], paired(n2[pair][:, :, :VH]), -1.0, paired(t1[:, planes, :VH]), MULT, MIN)
            nc.vector.scalar_tensor_tensor(hi0[:, pair], paired(n2[pair][:, :, :VH]), -1.0, paired(t1[:, planes, :VH]), MULT, MAX)
        nc.vector.tensor_tensor(mid0[:], t3[0][:].rearrange("p (a e) v -> p a v e", e=2), lo0[:], MAX)
        for pair in range(2):
            planes = slice(2 * pair, 2 * pair + 2)
            nc.vector.scalar_tensor_tensor(n3[:, pair], paired(sg3_sb[:, planes, :VH]), -1.0, paired(sg3_sb[:, planes, VH:]), MULT, MULT)
        nc.vector.tensor_tensor(z_bf[0][:].rearrange("p v (a e) -> p v a e", e=2), by_key(mid0[:]), by_key(hi0[:]), MIN)
        for pair in range(2):
            planes = slice(2 * pair, 2 * pair + 2)
            nc.vector.scalar_tensor_tensor(mid1[:, pair], paired(hi_ps[:, planes]), -1.0, n3[:, pair], MULT, MAX)
        quantize_z(0, 0, VH)
        second_product(0, 0, 2, 2, nc.scalar.copy, nc.sync)
        quantize_w2(1, 0, NH)
        second_product(0, 2, 2, 4, nc.scalar.copy, nc.sync)
        for keys in quarters:
            nc.vector.tensor_tensor(
                z_bf[1][:, keys].rearrange("p v (a e) -> p v a e", e=2),
                nlo_ps[:, :, keys].rearrange("p (a e) v -> p v a e", e=2),
                by_key(mid1[:, :, keys]),
                MIN,
            )
        for keys in quarters:
            quantize_z(1, keys.start, keys.stop)

        def negate_on_scalar(dst, src):
            nc.scalar.activation(dst, src, COPY, scale=-1.0)

        def negate_on_vector(dst, src):
            nc.vector.tensor_scalar_mul(dst, src, -1.0)

        for u in range(PACK):
            if u % 2 == 0:
                second_product(1, u, 1, (3, 6, 5, 7)[u], negate_on_scalar, nc.scalar)
            else:
                second_product(1, u, 1, (3, 6, 5, 7)[u], negate_on_vector, nc.sync)
